import numpy as np
import ml_dtypes


def mxq(x, axis, fmt="e4m3"):
    dtype, down = {"e4m3": (ml_dtypes.float8_e4m3fn, 7), "e5m2": (ml_dtypes.float8_e5m2, 14)}[fmt]
    v = np.moveaxis(np.asarray(x, np.float32).astype(ml_dtypes.bfloat16).astype(np.float64), axis, -1)
    blocks = v.reshape(v.shape[:-1] + (-1, 32))
    amax = np.abs(blocks).max(-1, keepdims=True)
    byte = np.maximum(np.where(amax > 0, np.frexp(amax)[1] - 1 + 127, 0) - down, 1)
    scale = np.exp2(byte - 127.0)
    codes = (blocks / scale).astype(np.float32).astype(dtype).astype(np.float64)
    return np.moveaxis((codes * scale).reshape(v.shape), -1, axis)


WIDE = False


def mx_kscale(k):
    if not WIDE:
        return np.ones(k)
    levels = np.array([10, -10, 5, -5, 0])
    if k % 512:
        return np.exp2(np.random.permutation(np.resize(levels, k // 32))).repeat(32)
    a = np.empty((k // 512, 16))
    for p in range(k // 512):
        a[p, :8] = np.random.permutation(np.resize(levels, 8))
        for g in range(8):
            far = levels[np.abs(levels - a[p, g]) >= 10]
            a[p, g + 8] = far[np.random.randint(len(far))]
    return np.exp2(a.ravel()).repeat(32)


def f64(x):
    return np.asarray(x).astype(np.float64)


def striped(idx):
    return np.tile(idx.reshape(-1, 16).T, (8, 1)).astype(np.uint16)


def unstriped(offs):
    return offs[:16].T.reshape(-1).astype(np.int64)


E2M1 = np.array([0.0, 0.5, 1.0, 1.5, 2.0, 3.0, 4.0, 6.0, -0.0, -0.5, -1.0, -1.5, -2.0, -3.0, -4.0, -6.0])


def pack_weight(w, fmt):
    k, n = w.shape
    w = f64(np.asarray(w, np.float32).astype(ml_dtypes.bfloat16)).reshape(k // 32, 32, n)
    amax = np.abs(w).max(1)
    if fmt == "e4m3":
        byte = np.frexp(amax)[1] - 1 + 127 - 7
    else:
        mant, ex = np.frexp(amax / 6.0)
        byte = np.where(mant > 0.5, ex, ex - 1) + 127
    byte = np.clip(np.where(amax > 0, byte, 1), 1, 254)
    scaled = (w * np.exp2(127.0 - byte)[:, None, :]).reshape(k, n).astype(np.float32)
    by_word = np.ascontiguousarray(scaled.reshape(k // 512, 128, 4, n).transpose(0, 1, 3, 2))
    if fmt == "e4m3":
        words = by_word.astype(ml_dtypes.float8_e4m3fn).view(np.uint8)
    else:
        c = by_word.astype(ml_dtypes.float4_e2m1fn).view(np.uint8) & 0xF
        words = (c[..., 0::2] | (c[..., 1::2] << 4)).reshape(k // 512, 128, 2 * n)
    return np.ascontiguousarray(words), np.ascontiguousarray(byte.astype(np.uint8).reshape(k // 512, 16, n))


def unpack_weight(words, scales, fmt):
    g, _, n = scales.shape
    words = np.ascontiguousarray(words).reshape(g, 128, n, -1)
    if fmt == "e4m3":
        vals = words.view(ml_dtypes.float8_e4m3fn).astype(np.float64)
    else:
        nib = np.empty((g, 128, n, 4), np.uint8)
        nib[..., 0::2] = words & 0xF
        nib[..., 1::2] = words >> 4
        vals = E2M1[nib]
    vals = vals * np.repeat(np.exp2(scales.astype(np.float64) - 127.0), 8, axis=1)[..., None]
    return vals.transpose(0, 1, 3, 2).reshape(g * 512, n)


def gelu(v):
    return 0.5 * v * (1.0 + np.tanh(np.sqrt(2.0 / np.pi) * (v + 0.044715 * v**3)))


K, T, S, H, T2, S2 = 1536, 2048, 512, 1024, 4096, 1024

def setup_inputs():
    n = np.random.standard_normal
    s = mx_kscale(K)[:, None]
    u = mx_kscale(H)[:, None]
    tab_words, tab_scales = pack_weight(n((K, T)) * s, "e4m3")
    tab2_words, tab2_scales = pack_weight(n((H, T2)) / np.sqrt(H) / u, "e4m3")
    w4_words, w4_scales = pack_weight(2.0 * n((K, H)) / np.sqrt(K) / s * u.T, "e2m1")
    return {
        "tab_words": tab_words, "tab_scales": tab_scales,
        "offs": striped(np.random.permutation(T)[:S]),
        "tab2_words": tab2_words, "tab2_scales": tab2_scales,
        "offs2": striped(np.random.permutation(T2)[:S2]),
        "w1": (0.4 * n((K, H)) / np.sqrt(K) / s).astype(np.float32),
        "b1": np.random.uniform(-0.5, 0.5, H).astype(np.float32),
        "w4_words": w4_words, "w4_scales": w4_scales,
        "mask": np.random.uniform(0.2, 1.0, S2).astype(np.float32),
        "bval": (0.5 * n(S2)).astype(np.float32),
    }

def reference(tab_words, tab_scales, offs, tab2_words, tab2_scales, offs2, w1, b1, w4_words, w4_scales, mask, bval):
    v = unpack_weight(tab_words, tab_scales, "e4m3")[:, unstriped(offs)]
    v2 = unpack_weight(tab2_words, tab2_scales, "e4m3")[:, unstriped(offs2)]
    w4 = unpack_weight(w4_words, w4_scales, "e2m1")
    amp = w4.T @ v
    phase = (mxq(f64(w1), 0, "e4m3").T @ v) + f64(b1)[:, None]
    h = amp * np.sin(phase)
    y = v2.T @ mxq(h, 0, "e4m3")
    return y * f64(mask)[:, None] + f64(bval)[:, None]

@@ -1,0 +1,357 @@
+from contextlib import ExitStack
+
+import concourse.mybir as mybir
+from concourse.masks import make_identity
+
+K, T, S, H, T2, S2 = 1536, 2048, 512, 1024, 4096, 1024
+FLOPS = 2 * (2 * K * H * S + H * S2 * S)
+
+F32 = mybir.dt.float32
+BF16 = mybir.dt.bfloat16
+I32 = mybir.dt.int32
+U32 = mybir.dt.uint32
+U16 = mybir.dt.uint16
+U8 = mybir.dt.uint8
+FP8X4 = mybir.dt.float8_e4m3fn_x4
+FP4X4 = mybir.dt.float4_e2m1fn_x4
+ACT = mybir.ActivationFunctionType
+ALU = mybir.AluOpType
+
+P = 128
+PASS = 512
+KA = K // PASS
+HB = H // PASS
+NT = S2 // P
+
+
+def tile_list_mesh_deeponet_sine_kernel(
+    tc, tab_words, tab_scales, offs, tab2_words, tab2_scales, offs2, w1, b1, w4_words, w4_scales, mask, bval, out
+):
+    nc = tc.nc
+    with ExitStack() as ctx:
+        keep = ctx.enter_context(tc.tile_pool(name="keep", bufs=1))
+        psum = ctx.enter_context(tc.psum_pool(name="psum", bufs=1))
+
+        def sb(name, shape, dtype):
+            return keep.tile(shape, dtype, name=name, align_bytes=64)
+
+        def bank(n, name):
+            return psum.tile([P, PASS], F32, name=name, tag="bank%d" % n)
+
+        offs_t = keep.tile([P, S // 16], U16, name="offs_t")
+        offs2_t = keep.tile([P, S2 // 16], U16, name="offs2_t")
+        bias = sb("bias", [P, HB, 4], F32)
+        rows = sb("rows", [P, P], F32)
+        ident = sb("ident", [P, P], F32)
+        cols = sb("cols", [P, 2 * NT], F32)
+        warm = sb("warm", [P, 8], F32)
+
+        tab_win = [sb("tab_win%d" % a, [P, T], I32) for a in range(KA)]
+        tabs_win = sb("tabs_win", [P, KA, T // 4], I32)
+        tab2_win = [sb("tab2_win%d" % b, [P, T2], I32) for b in range(HB)]
+        tab2s_win = sb("tab2s_win", [P, T2 // 4], I32)
+        w4_raw = [sb("w4_raw%d" % b, [P, KA, PASS // 2], I32) for b in range(HB)]
+        w4s_raw = sb("w4s_raw", [P, KA, H // 4], I32)
+        w1_raw = [[sb("w1_raw%d%d" % (a, b), [P, 4, PASS], F32) for b in range(HB)] for a in range(KA)]
+
+        v_w = [sb("v_w%d" % a, [P, S], U32) for a in range(KA)]
+        v_s = [sb("v_s%d" % a, [P, S], U8) for a in range(KA)]
+        v2_w = [sb("v2_w%d" % b, [P, S2], U32) for b in range(HB)]
+        v2_s = sb("v2_s", [P, S2], U8)
+        w4_w = [sb("w4_w%d" % b, [P, KA, 2 * PASS], U8) for b in range(HB)]
+        w4_s = [sb("w4_s%d" % b, [P, KA, PASS], U8) for b in range(HB)]
+        w1_bf = [[sb("w1_bf%d%d" % (a, b), [P, 4 * PASS], BF16) for b in range(HB)] for a in range(KA)]
+        w1_w = [[sb("w1_w%d%d" % (a, b), [P, PASS], U32) for b in range(HB)] for a in range(KA)]
+        w1_s = [[sb("w1_s%d%d" % (a, b), [P, PASS], U8) for b in range(HB)] for a in range(KA)]
+        sine = [sb("sine%d" % b, [P, 4, S], F32) for b in range(HB)]
+        h_bf = [sb("h_bf%d" % b, [P, 4 * S], BF16) for b in range(HB)]
+        h_w = [sb("h_w%d" % b, [P, S], U32) for b in range(HB)]
+        h_s = [sb("h_s%d" % b, [P, S], U8) for b in range(HB)]
+        res = [sb("res%d" % c, [P, S], F32) for c in range(NT)]
+
+        nc.gpsimd.memset(rows[:], 0.0)
+        nc.gpsimd.memset(tabs_win[:, 0, :], 0)
+        nc.vector.memset(tabs_win[:, 1:, :], 0)
+        nc.vector.memset(w4s_raw[:], 0)
+        nc.vector.memset(tab2s_win[:], 0)
+        nc.gpsimd.memset(warm[:], 0.0)
+        make_identity(nc, ident[:])
+        nc.scalar.activation(warm[:, 4:5], warm[:, 0:1], ACT.Sin)
+
+        def load_w1(a, b):
+            src = w1[a * PASS : (a + 1) * PASS, b * PASS : (b + 1) * PASS]
+            nc.sync.dma_start(w1_raw[a][b][:], src.rearrange("(p j) c -> p j c", j=4))
+
+        def load_w4(b):
+            src = w4_words.rearrange("a p n -> p a n")[:, :, 2 * b * PASS : 2 * (b + 1) * PASS]
+            nc.sync.dma_start(w4_raw[b][:], src.bitcast(I32))
+
+        def load_words(win, words):
+            nc.sync.dma_start(win[:], words.rearrange("p t i -> p (t i)").bitcast(I32))
+
+        def load_scale_rows(win, scales, r):
+            src = scales.rearrange("a (q r) t -> r q a t", r=4)[r]
+            nc.sync.dma_start(win[r:P:32], src.bitcast(I32))
+
+        def load_tab2_scale_rows(b, r):
+            src = tab2_scales[b].rearrange("(q r) t -> r q t", r=4)[r]
+            nc.sync.dma_start(tab2s_win[4 * (b + 1) + r : P : 32], src.bitcast(I32))
+
+        def permute_w4_words(b):
+            nc.vector.tensor_copy(
+                w4_w[b][:].bitcast(U16).rearrange("p a (t m) -> p t a m", t=4),
+                w4_raw[b][:].bitcast(U16).rearrange("p a (m t) -> p t a m", t=4),
+            )
+
+        def permute_w4_scales(b):
+            nc.vector.tensor_copy(
+                w4_s[b][:].rearrange("p a (t m) -> p t a m", t=4),
+                w4s_raw[:, :, b * 128 : (b + 1) * 128].bitcast(U8).rearrange("p a (m t) -> p t a m", t=4),
+            )
+
+        def gather_tab_scales(a):
+            nc.vector.tensor_copy(v_s[a][:], tabs_win[:, a, :].bitcast(U8).indirect(offs_t[:]))
+
+        def gather_tab_words(a):
+            nc.vector.tensor_copy(v_w[a][:], tab_win[a][:].bitcast(U32).indirect(offs_t[:]))
+
+        def gather_tab2_words(b, half):
+            nc.vector.tensor_copy(
+                v2_w[b][:, half * 512 : (half + 1) * 512],
+                tab2_win[b][:].bitcast(U32).indirect(offs2_t[:, half * 32 : (half + 1) * 32]),
+            )
+
+        def cast_w1(copy, a, b, t0, t1):
+            copy(
+                w1_bf[a][b][:].rearrange("p (t m j) -> p m j t", t=4, j=4)[:, :, :, t0:t1],
+                w1_raw[a][b][:].rearrange("p j (m t) -> p m j t", t=4)[:, :, :, t0:t1],
+            )
+
+        def quantize_w1(a, b, t0, t1):
+            m = slice(t0 * P, t1 * P)
+            nc.vector.quantize_mx(
+                w1_w[a][b][:, m].bitcast(FP8X4), w1_s[a][b][:, m], w1_bf[a][b][:, t0 * PASS : t1 * PASS]
+            )
+
+        def gather_tab2_scales(half):
+            nc.vector.tensor_copy(
+                v2_s[:, half * 512 : (half + 1) * 512],
+                tab2s_win[:].bitcast(U8).indirect(offs2_t[:, half * 32 : (half + 1) * 32]),
+            )
+
+        def phase_pass(acc, a, b, t):
+            m = slice(t * P, (t + 1) * P)
+            nc.tensor.matmul_mx(
+                acc[:],
+                lhsT=w1_w[a][b][:, m].bitcast(FP8X4),
+                lhsT_scale=w1_s[a][b][:, m],
+                rhs=v_w[a][:].bitcast(FP8X4),
+                rhs_scale=v_s[a][:],
+                start=(a == 0),
+                stop=(a == KA - 1),
+            )
+
+        def amp_bank(acc, b, jc):
+            j = slice(jc * P, (jc + 1) * P)
+            for t in range(4):
+                c0 = t * P
+                for a in range(KA):
+                    nc.tensor.matmul_mx(
+                        acc[:, t * P : (t + 1) * P],
+                        lhsT=w4_w[b][:, a, 2 * c0 : 2 * (c0 + P)].bitcast(FP4X4),
+                        lhsT_scale=w4_s[b][:, a, c0 : c0 + P],
+                        rhs=v_w[a][:, j].bitcast(FP8X4),
+                        rhs_scale=v_s[a][:, j],
+                        start=(a == 0),
+                        stop=(a == KA - 1),
+                    )
+
+        def sine_of(acc, b, t, half):
+            j = slice(half * 256, (half + 1) * 256)
+            nc.scalar.activation(sine[b][:, t, j], acc[:, j], ACT.Sin, bias=bias[:, b, t : t + 1])
+
+        def product(acc, b, jc):
+            nc.vector.tensor_tensor(
+                h_bf[b][:, jc * PASS : (jc + 1) * PASS].rearrange("p (c i t) -> p c t i", i=4, t=4),
+                acc[:].rearrange("p (t c i) -> p c t i", t=4, i=4),
+                sine[b][:, :, jc * P : (jc + 1) * P].rearrange("p t (c i) -> p c t i", i=4),
+                ALU.mult,
+            )
+
+        def quantize_h(b, h0, h1):
+            j = slice(h0 * 256, h1 * 256)
+            nc.vector.quantize_mx(
+                h_w[b][:, j].bitcast(FP8X4), h_s[b][:, j], h_bf[b][:, h0 * 1024 : h1 * 1024]
+            )
+
+        def out_pass(acc, b, c):
+            m = slice(c * P, (c + 1) * P)
+            nc.tensor.matmul_mx(
+                acc[:],
+                lhsT=v2_w[b][:, m].bitcast(FP8X4),
+                lhsT_scale=v2_s[4 * (b + 1) : P, m],
+                rhs=h_w[b][:].bitcast(FP8X4),
+                rhs_scale=h_s[b][:],
+                start=(b == 0),
+                stop=(b == HB - 1),
+            )
+
+        def phase_passes(acc, a, b):
+            for t in range(4):
+                phase_pass(acc[t], a, b, t)
+
+        def sines(acc, b, half):
+            for t in range(4):
+                sine_of(acc[t], b, t, half)
+
+        on_scalar, on_vector = nc.scalar.copy, nc.vector.tensor_copy
+
+        def finish(c, vector):
+            scale, shift = cols[:, c : c + 1], cols[:, NT + c : NT + c + 1]
+            if vector:
+                nc.vector.tensor_scalar(res[c][:], acc[c][:], scale, shift, ALU.mult, ALU.add)
+            else:
+                nc.scalar.activation(res[c][:], acc[c][:], ACT.Identity, bias=shift, scale=scale)
+            nc.sync.dma_start(out[c * P : (c + 1) * P, :], res[c][:])
+
+        phase, amp, acc = {}, {}, {}
+        nc.sync.dma_start(offs_t[:], offs)
+        nc.sync.dma_start(bias[:], b1.rearrange("(b p t) -> p b t", b=HB, t=4))
+        nc.sync.dma_start(offs2_t[:], offs2)
+        load_w4(0)
+        nc.sync.dma_start(rows[0:NT, :], mask.rearrange("(c p) -> c p", p=P))
+        nc.sync.dma_start(rows[NT : 2 * NT, :], bval.rearrange("(c p) -> c p", p=P))
+        turned = bank(7, "turned")
+        nc.tensor.transpose(turned[:, 0:P], rows[:], ident[:])
+        nc.scalar.copy(cols[:], turned[:, 0 : 2 * NT])
+        load_w1(0, 0)
+        load_scale_rows(tabs_win, tab_scales, 0)
+        load_scale_rows(tabs_win, tab_scales, 1)
+        load_scale_rows(tabs_win, tab_scales, 2)
+        load_scale_rows(tabs_win, tab_scales, 3)
+        load_w1(1, 0)
+        load_scale_rows(w4s_raw, w4_scales, 0)
+        load_scale_rows(w4s_raw, w4_scales, 1)
+        load_words(tab_win[0], tab_words[0])
+        load_scale_rows(w4s_raw, w4_scales, 2)
+        load_scale_rows(w4s_raw, w4_scales, 3)
+        load_tab2_scale_rows(0, 0)
+        load_w1(2, 0)
+        load_tab2_scale_rows(0, 1)
+        load_tab2_scale_rows(0, 2)
+        load_tab2_scale_rows(0, 3)
+        load_words(tab_win[1], tab_words[1])
+        load_tab2_scale_rows(1, 0)
+        load_tab2_scale_rows(1, 1)
+        load_tab2_scale_rows(1, 2)
+        load_tab2_scale_rows(1, 3)
+        load_words(tab_win[2], tab_words[2])
+        load_w1(0, 1)
+        load_w4(1)
+        load_w1(1, 1)
+        load_w1(2, 1)
+        load_words(tab2_win[0], tab2_words[0])
+        load_words(tab2_win[1], tab2_words[1])
+        permute_w4_words(0)
+        gather_tab_scales(0)
+        gather_tab_scales(1)
+        gather_tab_scales(2)
+        cast_w1(on_scalar, 0, 0, 0, 4)
+        quantize_w1(0, 0, 0, 4)
+        cast_w1(on_scalar, 1, 0, 0, 4)
+        gather_tab_words(0)
+        phase[0] = [bank(t, "phase0%d" % t) for t in range(4)]
+        phase_passes(phase[0], 0, 0)
+        quantize_w1(1, 0, 0, 4)
+        permute_w4_scales(0)
+        permute_w4_scales(1)
+        cast_w1(on_scalar, 2, 0, 0, 4)
+        gather_tab_words(1)
+        phase_passes(phase[0], 1, 0)
+        quantize_w1(2, 0, 0, 4)
+        gather_tab2_scales(0)
+        gather_tab_words(2)
+        phase_passes(phase[0], 2, 0)
+        gather_tab2_scales(1)
+        cast_w1(on_vector, 0, 1, 0, 2)
+        cast_w1(on_scalar, 0, 1, 2, 4)
+        sines(phase[0], 0, 0)
+        amp[0, 0] = bank(4, "amp00")
+        amp_bank(amp[0, 0], 0, 0)
+        amp[0, 1] = bank(5, "amp01")
+        amp_bank(amp[0, 1], 0, 1)
+        amp[0, 2] = bank(6, "amp02")
+        amp_bank(amp[0, 2], 0, 2)
+        amp[0, 3] = bank(7, "amp03")
+        amp_bank(amp[0, 3], 0, 3)
+        permute_w4_words(1)
+        quantize_w1(0, 1, 0, 4)
+        product(amp[0, 0], 0, 0)
+        product(amp[0, 1], 0, 1)
+        sines(phase[0], 0, 1)
+        cast_w1(on_scalar, 1, 1, 0, 2)
+        cast_w1(on_vector, 1, 1, 2, 4)
+        product(amp[0, 2], 0, 2)
+        quantize_w1(1, 1, 0, 4)
+        cast_w1(on_scalar, 2, 1, 0, 2)
+        cast_w1(on_vector, 2, 1, 2, 4)
+        product(amp[0, 3], 0, 3)
+        quantize_w1(2, 1, 2, 4)
+        quantize_w1(2, 1, 0, 2)
+        phase[1] = [bank(t, "phase1%d" % t) for t in range(4)]
+        phase_passes(phase[1], 0, 1)
+        amp[1, 0] = bank(4, "amp10")
+        amp_bank(amp[1, 0], 1, 0)
+        phase_passes(phase[1], 1, 1)
+        phase_passes(phase[1], 2, 1)
+        amp[1, 1] = bank(5, "amp11")
+        amp_bank(amp[1, 1], 1, 1)
+        amp[1, 2] = bank(6, "amp12")
+        amp_bank(amp[1, 2], 1, 2)
+        amp[1, 3] = bank(7, "amp13")
+        amp_bank(amp[1, 3], 1, 3)
+        quantize_h(0, 0, 2)
+        sines(phase[1], 1, 0)
+        sines(phase[1], 1, 1)
+        gather_tab2_words(0, 0)
+        product(amp[1, 0], 1, 0)
+        product(amp[1, 1], 1, 1)
+        product(amp[1, 2], 1, 2)
+        product(amp[1, 3], 1, 3)
+        quantize_h(1, 0, 1)
+        quantize_h(1, 1, 2)
+        acc[0] = bank(0, "acc0")
+        out_pass(acc[0], 0, 0)
+        acc[1] = bank(1, "acc1")
+        out_pass(acc[1], 0, 1)
+        acc[2] = bank(2, "acc2")
+        out_pass(acc[2], 0, 2)
+        acc[3] = bank(3, "acc3")
+        out_pass(acc[3], 0, 3)
+        gather_tab2_words(1, 0)
+        out_pass(acc[0], 1, 0)
+        out_pass(acc[1], 1, 1)
+        out_pass(acc[2], 1, 2)
+        out_pass(acc[3], 1, 3)
+        finish(0, False)
+        finish(1, False)
+        gather_tab2_words(0, 1)
+        acc[4] = bank(4, "acc4")
+        out_pass(acc[4], 0, 4)
+        acc[5] = bank(5, "acc5")
+        out_pass(acc[5], 0, 5)
+        acc[6] = bank(6, "acc6")
+        out_pass(acc[6], 0, 6)
+        acc[7] = bank(7, "acc7")
+        out_pass(acc[7], 0, 7)
+        gather_tab2_words(1, 1)
+        out_pass(acc[4], 1, 4)
+        out_pass(acc[5], 1, 5)
+        out_pass(acc[6], 1, 6)
+        out_pass(acc[7], 1, 7)
+        finish(2, False)
+        finish(3, False)
+        finish(4, False)
+        finish(5, True)
+        finish(6, False)
+        finish(7, True)

@@ -47,17 +47,19 @@ def tile_list_mesh_deeponet_sine_kernel(
         warm = sb("warm", [P, 8], F32)
 
         tab_win = [sb("tab_win%d" % a, [P, T], I32) for a in range(KA)]
-        tabs_win = sb("tabs_win", [P, KA, T // 4], I32)
+        tabs_win = sb("tabs_win", [P, T // 4], I32)
         tab2_win = [sb("tab2_win%d" % b, [P, T2], I32) for b in range(HB)]
         tab2s_win = sb("tab2s_win", [P, T2 // 4], I32)
-        w4_raw = [sb("w4_raw%d" % b, [P, KA, PASS // 2], I32) for b in range(HB)]
+        w4_raw = sb("w4_raw", [P, KA, H // 2], I32)
         w4s_raw = sb("w4s_raw", [P, KA, H // 4], I32)
         w1_raw = [[sb("w1_raw%d%d" % (a, b), [P, 4, PASS], F32) for b in range(HB)] for a in range(KA)]
 
         v_w = [sb("v_w%d" % a, [P, S], U32) for a in range(KA)]
-        v_s = [sb("v_s%d" % a, [P, S], U8) for a in range(KA)]
+        v_sg = sb("v_sg", [P, S], U8)
+        v_s = sb("v_s", [P, 4, S // 4], I32)
         v2_w = [sb("v2_w%d" % b, [P, S2], U32) for b in range(HB)]
-        v2_s = sb("v2_s", [P, S2], U8)
+        v2_sg = sb("v2_sg", [P, S2], U8)
+        v2_s = sb("v2_s", [P, HB, S2 // 4], I32)
         w4_w = [sb("w4_w%d" % b, [P, KA, 2 * PASS], U8) for b in range(HB)]
         w4_s = [sb("w4_s%d" % b, [P, KA, PASS], U8) for b in range(HB)]
         w1_bf = [[sb("w1_bf%d%d" % (a, b), [P, 4 * PASS], BF16) for b in range(HB)] for a in range(KA)]
@@ -69,11 +71,12 @@ def tile_list_mesh_deeponet_sine_kernel(
         h_s = [sb("h_s%d" % b, [P, S], U8) for b in range(HB)]
         res = [sb("res%d" % c, [P, S], F32) for c in range(NT)]
 
-        nc.gpsimd.memset(rows[:], 0.0)
-        nc.gpsimd.memset(tabs_win[:, 0, :], 0)
-        nc.vector.memset(tabs_win[:, 1:, :], 0)
+        nc.gpsimd.memset(tabs_win[:], 0)
         nc.vector.memset(w4s_raw[:], 0)
         nc.vector.memset(tab2s_win[:], 0)
+        nc.vector.memset(v_s[:], 0)
+        nc.vector.memset(v2_s[:], 0)
+        nc.gpsimd.memset(rows[:], 0.0)
         nc.gpsimd.memset(warm[:], 0.0)
         make_identity(nc, ident[:])
         nc.scalar.activation(warm[:, 4:5], warm[:, 0:1], ACT.Sin)
@@ -82,25 +85,29 @@ def tile_list_mesh_deeponet_sine_kernel(
             src = w1[a * PASS : (a + 1) * PASS, b * PASS : (b + 1) * PASS]
             nc.sync.dma_start(w1_raw[a][b][:], src.rearrange("(p j) c -> p j c", j=4))
 
-        def load_w4(b):
-            src = w4_words.rearrange("a p n -> p a n")[:, :, 2 * b * PASS : 2 * (b + 1) * PASS]
-            nc.sync.dma_start(w4_raw[b][:], src.bitcast(I32))
-
         def load_words(win, words):
             nc.sync.dma_start(win[:], words.rearrange("p t i -> p (t i)").bitcast(I32))
 
         def load_scale_rows(win, scales, r):
             src = scales.rearrange("a (q r) t -> r q a t", r=4)[r]
-            nc.sync.dma_start(win[r:P:32], src.bitcast(I32))
+            nc.gpsimd.dma_start(win[r:P:32], src.bitcast(I32))
 
-        def load_tab2_scale_rows(b, r):
-            src = tab2_scales[b].rearrange("(q r) t -> r q t", r=4)[r]
-            nc.sync.dma_start(tab2s_win[4 * (b + 1) + r : P : 32], src.bitcast(I32))
+        def load_tab2_scale_rows(b):
+            nc.sync.dma_start(tab2s_win[4 * b : P : 8], tab2_scales[b].bitcast(I32))
+
+        def move_tab2_scale_rows(q):
+            nc.gpsimd.dma_start(v2_s[32 * q + 4 : 32 * q + 8], v2_sg[32 * q : 32 * (q + 1) : 4].bitcast(I32))
+
+        def load_tab_scale_rows(a):
+            nc.sync.dma_start(tabs_win[2 * a : P : 8], tab_scales[a].bitcast(I32))
+
+        def move_tab_scale_rows(q):
+            nc.sync.dma_start(v_s[32 * q : 32 * q + 4], v_sg[32 * q : 32 * (q + 1) : 2].bitcast(I32))
 
         def permute_w4_words(b):
             nc.vector.tensor_copy(
                 w4_w[b][:].bitcast(U16).rearrange("p a (t m) -> p t a m", t=4),
-                w4_raw[b][:].bitcast(U16).rearrange("p a (m t) -> p t a m", t=4),
+                w4_raw[:, :, b * 256 : (b + 1) * 256].bitcast(U16).rearrange("p a (m t) -> p t a m", t=4),
             )
 
         def permute_w4_scales(b):
@@ -109,8 +116,8 @@ def tile_list_mesh_deeponet_sine_kernel(
                 w4s_raw[:, :, b * 128 : (b + 1) * 128].bitcast(U8).rearrange("p a (m t) -> p t a m", t=4),
             )
 
-        def gather_tab_scales(a):
-            nc.vector.tensor_copy(v_s[a][:], tabs_win[:, a, :].bitcast(U8).indirect(offs_t[:]))
+        def gather_tab_scales():
+            nc.vector.tensor_copy(v_sg[:], tabs_win[:].bitcast(U8).indirect(offs_t[:]))
 
         def gather_tab_words(a):
             nc.vector.tensor_copy(v_w[a][:], tab_win[a][:].bitcast(U32).indirect(offs_t[:]))
@@ -133,11 +140,8 @@ def tile_list_mesh_deeponet_sine_kernel(
                 w1_w[a][b][:, m].bitcast(FP8X4), w1_s[a][b][:, m], w1_bf[a][b][:, t0 * PASS : t1 * PASS]
             )
 
-        def gather_tab2_scales(half):
-            nc.vector.tensor_copy(
-                v2_s[:, half * 512 : (half + 1) * 512],
-                tab2s_win[:].bitcast(U8).indirect(offs2_t[:, half * 32 : (half + 1) * 32]),
-            )
+        def gather_tab2_scales():
+            nc.vector.tensor_copy(v2_sg[:], tab2s_win[:].bitcast(U8).indirect(offs2_t[:]))
 
         def phase_pass(acc, a, b, t):
             m = slice(t * P, (t + 1) * P)
@@ -146,7 +150,7 @@ def tile_list_mesh_deeponet_sine_kernel(
                 lhsT=w1_w[a][b][:, m].bitcast(FP8X4),
                 lhsT_scale=w1_s[a][b][:, m],
                 rhs=v_w[a][:].bitcast(FP8X4),
-                rhs_scale=v_s[a][:],
+                rhs_scale=v_s[:, a, :].bitcast(U8),
                 start=(a == 0),
                 stop=(a == KA - 1),
             )
@@ -161,7 +165,7 @@ def tile_list_mesh_deeponet_sine_kernel(
                         lhsT=w4_w[b][:, a, 2 * c0 : 2 * (c0 + P)].bitcast(FP4X4),
                         lhsT_scale=w4_s[b][:, a, c0 : c0 + P],
                         rhs=v_w[a][:, j].bitcast(FP8X4),
-                        rhs_scale=v_s[a][:, j],
+                        rhs_scale=v_s[:, a, :].bitcast(U8)[:, j],
                         start=(a == 0),
                         stop=(a == KA - 1),
                     )
@@ -189,7 +193,7 @@ def tile_list_mesh_deeponet_sine_kernel(
             nc.tensor.matmul_mx(
                 acc[:],
                 lhsT=v2_w[b][:, m].bitcast(FP8X4),
-                lhsT_scale=v2_s[4 * (b + 1) : P, m],
+                lhsT_scale=v2_s[4:P, b, :].bitcast(U8)[:, m],
                 rhs=h_w[b][:].bitcast(FP8X4),
                 rhs_scale=h_s[b][:],
                 start=(b == 0),
@@ -216,66 +220,57 @@ def tile_list_mesh_deeponet_sine_kernel(
 
         phase, amp, acc = {}, {}, {}
         nc.sync.dma_start(offs_t[:], offs)
-        nc.sync.dma_start(bias[:], b1.rearrange("(b p t) -> p b t", b=HB, t=4))
         nc.sync.dma_start(offs2_t[:], offs2)
-        load_w4(0)
+        for a in range(KA):
+            load_tab_scale_rows(a)
+        nc.sync.dma_start(w4_raw[:], w4_words.rearrange("a p n -> p a n").bitcast(I32))
+        load_w1(0, 0)
+        for b in range(HB):
+            load_tab2_scale_rows(b)
+        load_w1(1, 0)
         nc.sync.dma_start(rows[0:NT, :], mask.rearrange("(c p) -> c p", p=P))
         nc.sync.dma_start(rows[NT : 2 * NT, :], bval.rearrange("(c p) -> c p", p=P))
-        turned = bank(7, "turned")
-        nc.tensor.transpose(turned[:, 0:P], rows[:], ident[:])
-        nc.scalar.copy(cols[:], turned[:, 0 : 2 * NT])
-        load_w1(0, 0)
-        load_scale_rows(tabs_win, tab_scales, 0)
-        load_scale_rows(tabs_win, tab_scales, 1)
-        load_scale_rows(tabs_win, tab_scales, 2)
-        load_scale_rows(tabs_win, tab_scales, 3)
-        load_w1(1, 0)
-        load_scale_rows(w4s_raw, w4_scales, 0)
-        load_scale_rows(w4s_raw, w4_scales, 1)
         load_words(tab_win[0], tab_words[0])
-        load_scale_rows(w4s_raw, w4_scales, 2)
-        load_scale_rows(w4s_raw, w4_scales, 3)
-        load_tab2_scale_rows(0, 0)
         load_w1(2, 0)
-        load_tab2_scale_rows(0, 1)
-        load_tab2_scale_rows(0, 2)
-        load_tab2_scale_rows(0, 3)
+        for r in range(4):
+            load_scale_rows(w4s_raw, w4_scales, r)
+        nc.gpsimd.dma_start(bias[:], b1.rearrange("(b p t) -> p b t", b=HB, t=4))
+        gather_tab_scales()
+        for q in range(4):
+            move_tab_scale_rows(q)
         load_words(tab_win[1], tab_words[1])
-        load_tab2_scale_rows(1, 0)
-        load_tab2_scale_rows(1, 1)
-        load_tab2_scale_rows(1, 2)
-        load_tab2_scale_rows(1, 3)
         load_words(tab_win[2], tab_words[2])
         load_w1(0, 1)
-        load_w4(1)
         load_w1(1, 1)
         load_w1(2, 1)
         load_words(tab2_win[0], tab2_words[0])
         load_words(tab2_win[1], tab2_words[1])
         permute_w4_words(0)
-        gather_tab_scales(0)
-        gather_tab_scales(1)
-        gather_tab_scales(2)
+        permute_w4_words(1)
+        gather_tab2_scales()
+        for q in range(4):
+            move_tab2_scale_rows(q)
         cast_w1(on_scalar, 0, 0, 0, 4)
         quantize_w1(0, 0, 0, 4)
+        permute_w4_scales(0)
+        permute_w4_scales(1)
+        turned = bank(7, "turned")
+        nc.tensor.transpose(turned[:, 0:P], rows[:], ident[:])
+        nc.scalar.copy(cols[:], turned[:, 0 : 2 * NT])
         cast_w1(on_scalar, 1, 0, 0, 4)
         gather_tab_words(0)
         phase[0] = [bank(t, "phase0%d" % t) for t in range(4)]
         phase_passes(phase[0], 0, 0)
         quantize_w1(1, 0, 0, 4)
-        permute_w4_scales(0)
-        permute_w4_scales(1)
         cast_w1(on_scalar, 2, 0, 0, 4)
         gather_tab_words(1)
         phase_passes(phase[0], 1, 0)
         quantize_w1(2, 0, 0, 4)
-        gather_tab2_scales(0)
         gather_tab_words(2)
         phase_passes(phase[0], 2, 0)
-        gather_tab2_scales(1)
-        cast_w1(on_vector, 0, 1, 0, 2)
-        cast_w1(on_scalar, 0, 1, 2, 4)
+        cast_w1(on_vector, 0, 1, 0, 4)
         sines(phase[0], 0, 0)
+        sines(phase[0], 0, 1)
         amp[0, 0] = bank(4, "amp00")
         amp_bank(amp[0, 0], 0, 0)
         amp[0, 1] = bank(5, "amp01")
@@ -284,28 +279,26 @@ def tile_list_mesh_deeponet_sine_kernel(
         amp_bank(amp[0, 2], 0, 2)
         amp[0, 3] = bank(7, "amp03")
         amp_bank(amp[0, 3], 0, 3)
-        permute_w4_words(1)
-        quantize_w1(0, 1, 0, 4)
         product(amp[0, 0], 0, 0)
+        quantize_w1(0, 1, 0, 4)
         product(amp[0, 1], 0, 1)
-        sines(phase[0], 0, 1)
-        cast_w1(on_scalar, 1, 1, 0, 2)
         cast_w1(on_vector, 1, 1, 2, 4)
+        cast_w1(on_scalar, 1, 1, 0, 2)
         product(amp[0, 2], 0, 2)
-        quantize_w1(1, 1, 0, 4)
+        product(amp[0, 3], 0, 3)
         cast_w1(on_scalar, 2, 1, 0, 2)
         cast_w1(on_vector, 2, 1, 2, 4)
-        product(amp[0, 3], 0, 3)
+        quantize_w1(1, 1, 0, 4)
         quantize_w1(2, 1, 2, 4)
         quantize_w1(2, 1, 0, 2)
         phase[1] = [bank(t, "phase1%d" % t) for t in range(4)]
         phase_passes(phase[1], 0, 1)
         amp[1, 0] = bank(4, "amp10")
         amp_bank(amp[1, 0], 1, 0)
-        phase_passes(phase[1], 1, 1)
-        phase_passes(phase[1], 2, 1)
         amp[1, 1] = bank(5, "amp11")
         amp_bank(amp[1, 1], 1, 1)
+        phase_passes(phase[1], 1, 1)
+        phase_passes(phase[1], 2, 1)
         amp[1, 2] = bank(6, "amp12")
         amp_bank(amp[1, 2], 1, 2)
         amp[1, 3] = bank(7, "amp13")
@@ -320,13 +313,13 @@ def tile_list_mesh_deeponet_sine_kernel(
         product(amp[1, 3], 1, 3)
         quantize_h(1, 0, 1)
         quantize_h(1, 1, 2)
-        acc[0] = bank(0, "acc0")
+        acc[0] = bank(4 + 0, "acc0")
         out_pass(acc[0], 0, 0)
-        acc[1] = bank(1, "acc1")
+        acc[1] = bank(5 + 0, "acc1")
         out_pass(acc[1], 0, 1)
-        acc[2] = bank(2, "acc2")
+        acc[2] = bank(6 + 0, "acc2")
         out_pass(acc[2], 0, 2)
-        acc[3] = bank(3, "acc3")
+        acc[3] = bank(7 + 0, "acc3")
         out_pass(acc[3], 0, 3)
         gather_tab2_words(1, 0)
         out_pass(acc[0], 1, 0)
@@ -336,13 +329,13 @@ def tile_list_mesh_deeponet_sine_kernel(
         finish(0, False)
         finish(1, False)
         gather_tab2_words(0, 1)
-        acc[4] = bank(4, "acc4")
+        acc[4] = bank(0 + 0, "acc4")
         out_pass(acc[4], 0, 4)
-        acc[5] = bank(5, "acc5")
+        acc[5] = bank(1 + 0, "acc5")
         out_pass(acc[5], 0, 5)
-        acc[6] = bank(6, "acc6")
+        acc[6] = bank(2 + 0, "acc6")
         out_pass(acc[6], 0, 6)
-        acc[7] = bank(7, "acc7")
+        acc[7] = bank(3 + 0, "acc7")
         out_pass(acc[7], 0, 7)
         gather_tab2_words(1, 1)
         out_pass(acc[4], 1, 4)

@@ -22,6 +22,10 @@ PASS = 512
 KA = K // PASS
 HB = H // PASS
 NT = S2 // P
+ROWS = 16
+TS0 = P - KA * ROWS
+T2S0 = P - HB * ROWS
+R0 = P - 2 * NT
 
 
 def tile_list_mesh_deeponet_sine_kernel(
@@ -32,8 +36,8 @@ def tile_list_mesh_deeponet_sine_kernel(
         keep = ctx.enter_context(tc.tile_pool(name="keep", bufs=1))
         psum = ctx.enter_context(tc.psum_pool(name="psum", bufs=1))
 
-        def sb(name, shape, dtype):
-            return keep.tile(shape, dtype, name=name, align_bytes=64)
+        def sb(name, shape, dtype, tag=None):
+            return keep.tile(shape, dtype, name=name, tag=tag or name, align_bytes=64)
 
         def bank(n, name):
             return psum.tile([P, PASS], F32, name=name, tag="bank%d" % n)
@@ -56,7 +60,7 @@ def tile_list_mesh_deeponet_sine_kernel(
 
         v_w = [sb("v_w%d" % a, [P, S], U32) for a in range(KA)]
         v_sg = sb("v_sg", [P, S], U8)
-        v_s = sb("v_s", [P, 4, S // 4], I32)
+        v_s = sb("v_s", [P, KA, S // 4], I32)
         v2_w = [sb("v2_w%d" % b, [P, S2], U32) for b in range(HB)]
         v2_sg = sb("v2_sg", [P, S2], U8)
         v2_s = sb("v2_s", [P, HB, S2 // 4], I32)
@@ -66,20 +70,9 @@ def tile_list_mesh_deeponet_sine_kernel(
         w1_w = [[sb("w1_w%d%d" % (a, b), [P, PASS], U32) for b in range(HB)] for a in range(KA)]
         w1_s = [[sb("w1_s%d%d" % (a, b), [P, PASS], U8) for b in range(HB)] for a in range(KA)]
         sine = [sb("sine%d" % b, [P, 4, S], F32) for b in range(HB)]
-        h_bf = [sb("h_bf%d" % b, [P, 4 * S], BF16) for b in range(HB)]
         h_w = [sb("h_w%d" % b, [P, S], U32) for b in range(HB)]
         h_s = [sb("h_s%d" % b, [P, S], U8) for b in range(HB)]
         res = [sb("res%d" % c, [P, S], F32) for c in range(NT)]
-
-        nc.gpsimd.memset(tabs_win[:], 0)
-        nc.vector.memset(w4s_raw[:], 0)
-        nc.vector.memset(tab2s_win[:], 0)
-        nc.vector.memset(v_s[:], 0)
-        nc.vector.memset(v2_s[:], 0)
-        nc.gpsimd.memset(rows[:], 0.0)
-        nc.gpsimd.memset(warm[:], 0.0)
-        make_identity(nc, ident[:])
-        nc.scalar.activation(warm[:, 4:5], warm[:, 0:1], ACT.Sin)
 
         def load_w1(a, b):
             src = w1[a * PASS : (a + 1) * PASS, b * PASS : (b + 1) * PASS]
@@ -88,21 +81,17 @@ def tile_list_mesh_deeponet_sine_kernel(
         def load_words(win, words):
             nc.sync.dma_start(win[:], words.rearrange("p t i -> p (t i)").bitcast(I32))
 
-        def load_scale_rows(win, scales, r):
-            src = scales.rearrange("a (q r) t -> r q a t", r=4)[r]
-            nc.gpsimd.dma_start(win[r:P:32], src.bitcast(I32))
-
-        def load_tab2_scale_rows(b):
-            nc.sync.dma_start(tab2s_win[4 * b : P : 8], tab2_scales[b].bitcast(I32))
-
-        def move_tab2_scale_rows(q):
-            nc.gpsimd.dma_start(v2_s[32 * q + 4 : 32 * q + 8], v2_sg[32 * q : 32 * (q + 1) : 4].bitcast(I32))
-
-        def load_tab_scale_rows(a):
-            nc.sync.dma_start(tabs_win[2 * a : P : 8], tab_scales[a].bitcast(I32))
+        def load_w4_scale_rows(r):
+            src = w4_scales.rearrange("a (q r) t -> r q a t", r=4)[r]
+            nc.sync.dma_start(w4s_raw[r:P:32], src.bitcast(I32))
 
         def move_tab_scale_rows(q):
-            nc.sync.dma_start(v_s[32 * q : 32 * q + 4], v_sg[32 * q : 32 * (q + 1) : 2].bitcast(I32))
+            first = TS0 + 4 * KA * q
+            nc.sync.dma_start(v_s[32 * q : 32 * q + 4], v_sg[first : first + 4 * KA].bitcast(I32))
+
+        def move_tab2_scale_rows(q):
+            first = T2S0 + 4 * HB * q
+            nc.sync.dma_start(v2_s[32 * q + 4 : 32 * q + 8], v2_sg[first : first + 4 * HB].bitcast(I32))
 
         def permute_w4_words(b):
             nc.vector.tensor_copy(
@@ -122,71 +111,76 @@ def tile_list_mesh_deeponet_sine_kernel(
         def gather_tab_words(a):
             nc.vector.tensor_copy(v_w[a][:], tab_win[a][:].bitcast(U32).indirect(offs_t[:]))
 
+        def gather_tab2_scales():
+            nc.vector.tensor_copy(v2_sg[:], tab2s_win[:].bitcast(U8).indirect(offs2_t[:]))
+
         def gather_tab2_words(b, half):
             nc.vector.tensor_copy(
                 v2_w[b][:, half * 512 : (half + 1) * 512],
                 tab2_win[b][:].bitcast(U32).indirect(offs2_t[:, half * 32 : (half + 1) * 32]),
             )
 
-        def cast_w1(copy, a, b, t0, t1):
+        def cast_w1(copy, a, b, m0, m1):
             copy(
-                w1_bf[a][b][:].rearrange("p (t m j) -> p m j t", t=4, j=4)[:, :, :, t0:t1],
-                w1_raw[a][b][:].rearrange("p j (m t) -> p m j t", t=4)[:, :, :, t0:t1],
+                w1_bf[a][b][:].rearrange("p (t m j) -> p m j t", t=4, j=4)[:, m0:m1],
+                w1_raw[a][b][:].rearrange("p j (m t) -> p m j t", t=4)[:, m0:m1],
             )
 
-        def quantize_w1(a, b, t0, t1):
-            m = slice(t0 * P, t1 * P)
-            nc.vector.quantize_mx(
-                w1_w[a][b][:, m].bitcast(FP8X4), w1_s[a][b][:, m], w1_bf[a][b][:, t0 * PASS : t1 * PASS]
-            )
+        def quantize_w1(a, b):
+            nc.vector.quantize_mx(w1_w[a][b][:].bitcast(FP8X4), w1_s[a][b][:], w1_bf[a][b][:])
 
-        def gather_tab2_scales():
-            nc.vector.tensor_copy(v2_sg[:], tab2s_win[:].bitcast(U8).indirect(offs2_t[:]))
+        def phase_passes(acc, a, b):
+            for t in range(4):
+                m = slice(t * P, (t + 1) * P)
+                nc.tensor.matmul_mx(
+                    acc[t][:],
+                    lhsT=w1_w[a][b][:, m].bitcast(FP8X4),
+                    lhsT_scale=w1_s[a][b][:, m],
+                    rhs=v_w[a][:].bitcast(FP8X4),
+                    rhs_scale=v_s[:, a, :].bitcast(U8),
+                    start=(a == 0),
+                    stop=(a == KA - 1),
+                )
 
-        def phase_pass(acc, a, b, t):
-            m = slice(t * P, (t + 1) * P)
+        def amp_pass(dst, a, b, t, j):
+            c0 = t * P
             nc.tensor.matmul_mx(
-                acc[:],
-                lhsT=w1_w[a][b][:, m].bitcast(FP8X4),
-                lhsT_scale=w1_s[a][b][:, m],
-                rhs=v_w[a][:].bitcast(FP8X4),
-                rhs_scale=v_s[:, a, :].bitcast(U8),
+                dst,
+                lhsT=w4_w[b][:, a, 2 * c0 : 2 * (c0 + P)].bitcast(FP4X4),
+                lhsT_scale=w4_s[b][:, a, c0 : c0 + P],
+                rhs=v_w[a][:, j].bitcast(FP8X4),
+                rhs_scale=v_s[:, a, :].bitcast(U8)[:, j],
                 start=(a == 0),
                 stop=(a == KA - 1),
             )
 
-        def amp_bank(acc, b, jc):
-            j = slice(jc * P, (jc + 1) * P)
+        def amp_wide(acc, a, b):
             for t in range(4):
-                c0 = t * P
+                amp_pass(acc[t][:], a, b, t, slice(0, S))
+
+        def amp_bank(acc, b, jc):
+            for t in range(4):
                 for a in range(KA):
-                    nc.tensor.matmul_mx(
-                        acc[:, t * P : (t + 1) * P],
-                        lhsT=w4_w[b][:, a, 2 * c0 : 2 * (c0 + P)].bitcast(FP4X4),
-                        lhsT_scale=w4_s[b][:, a, c0 : c0 + P],
-                        rhs=v_w[a][:, j].bitcast(FP8X4),
-                        rhs_scale=v_s[:, a, :].bitcast(U8)[:, j],
-                        start=(a == 0),
-                        stop=(a == KA - 1),
-                    )
+                    amp_pass(acc[:, t * P : (t + 1) * P], a, b, t, slice(jc * P, (jc + 1) * P))
 
-        def sine_of(acc, b, t, half):
+        def sines(acc, b, half):
             j = slice(half * 256, (half + 1) * 256)
-            nc.scalar.activation(sine[b][:, t, j], acc[:, j], ACT.Sin, bias=bias[:, b, t : t + 1])
+            for t in range(4):
+                nc.scalar.activation(sine[b][:, t, j], acc[t][:, j], ACT.Sin, bias=bias[:, b, t : t + 1])
 
-        def product(acc, b, jc):
+        def product(dst, amp, b, j0, j1):
             nc.vector.tensor_tensor(
-                h_bf[b][:, jc * PASS : (jc + 1) * PASS].rearrange("p (c i t) -> p c t i", i=4, t=4),
-                acc[:].rearrange("p (t c i) -> p c t i", t=4, i=4),
-                sine[b][:, :, jc * P : (jc + 1) * P].rearrange("p t (c i) -> p c t i", i=4),
+                dst.rearrange("p (c i t) -> p c t i", i=4, t=4),
+                amp.rearrange("p t (c i) -> p c t i", i=4),
+                sine[b][:, :, j0:j1].rearrange("p t (c i) -> p c t i", i=4),
                 ALU.mult,
             )
 
-        def quantize_h(b, h0, h1):
-            j = slice(h0 * 256, h1 * 256)
-            nc.vector.quantize_mx(
-                h_w[b][:, j].bitcast(FP8X4), h_s[b][:, j], h_bf[b][:, h0 * 1024 : h1 * 1024]
-            )
+        def product_bank(dst, acc, b, jc):
+            product(dst, acc[:].rearrange("p (t j) -> p t j", t=4), b, jc * P, (jc + 1) * P)
+
+        def quantize_h(src, b, j0, j1):
+            nc.vector.quantize_mx(h_w[b][:, j0:j1].bitcast(FP8X4), h_s[b][:, j0:j1], src)
 
         def out_pass(acc, b, c):
             m = slice(c * P, (c + 1) * P)
@@ -200,151 +194,120 @@ def tile_list_mesh_deeponet_sine_kernel(
                 stop=(b == HB - 1),
             )
 
-        def phase_passes(acc, a, b):
-            for t in range(4):
-                phase_pass(acc[t], a, b, t)
-
-        def sines(acc, b, half):
-            for t in range(4):
-                sine_of(acc[t], b, t, half)
-
         on_scalar, on_vector = nc.scalar.copy, nc.vector.tensor_copy
 
-        def finish(c, vector):
+        def finish(acc, c, vector):
             scale, shift = cols[:, c : c + 1], cols[:, NT + c : NT + c + 1]
             if vector:
-                nc.vector.tensor_scalar(res[c][:], acc[c][:], scale, shift, ALU.mult, ALU.add)
+                nc.vector.tensor_scalar(res[c][:], acc[:], scale, shift, ALU.mult, ALU.add)
             else:
-                nc.scalar.activation(res[c][:], acc[c][:], ACT.Identity, bias=shift, scale=scale)
+                nc.scalar.activation(res[c][:], acc[:], ACT.Identity, bias=shift, scale=scale)
             nc.sync.dma_start(out[c * P : (c + 1) * P, :], res[c][:])
 
-        phase, amp, acc = {}, {}, {}
-        nc.sync.dma_start(offs_t[:], offs)
+        nc.vector.memset(tab2s_win[0:T2S0], 0)
+        nc.vector.memset(tabs_win[0:TS0], 0)
+        nc.vector.memset(v_s[:], 0)
+        nc.gpsimd.memset(warm[:], 0.0)
+        nc.gpsimd.memset(w4s_raw[:], 0)
+        nc.gpsimd.memset(v2_s[:], 0)
+        nc.gpsimd.memset(rows[0:R0], 0.0)
+        make_identity(nc, ident[:])
+        nc.scalar.activation(warm[:, 4:5], warm[:, 0:1], ACT.Sin)
+
         nc.sync.dma_start(offs2_t[:], offs2)
-        for a in range(KA):
-            load_tab_scale_rows(a)
-        nc.sync.dma_start(w4_raw[:], w4_words.rearrange("a p n -> p a n").bitcast(I32))
+        nc.sync.dma_start(tab2s_win[T2S0:P], tab2_scales.rearrange("b q t -> q b t").bitcast(I32))
         load_w1(0, 0)
-        for b in range(HB):
-            load_tab2_scale_rows(b)
-        load_w1(1, 0)
-        nc.sync.dma_start(rows[0:NT, :], mask.rearrange("(c p) -> c p", p=P))
-        nc.sync.dma_start(rows[NT : 2 * NT, :], bval.rearrange("(c p) -> c p", p=P))
+        nc.sync.dma_start(offs_t[:], offs)
+        nc.sync.dma_start(tabs_win[TS0:P], tab_scales.rearrange("a q t -> q a t").bitcast(I32))
+        nc.sync.dma_start(w4_raw[:], w4_words.rearrange("a p n -> p a n").bitcast(I32))
+        nc.sync.dma_start(bias[:], b1.rearrange("(b p t) -> p b t", b=HB, t=4))
+        nc.sync.dma_start(rows[R0 : R0 + NT, :], mask.rearrange("(c p) -> c p", p=P))
         load_words(tab_win[0], tab_words[0])
-        load_w1(2, 0)
         for r in range(4):
-            load_scale_rows(w4s_raw, w4_scales, r)
-        nc.gpsimd.dma_start(bias[:], b1.rearrange("(b p t) -> p b t", b=HB, t=4))
+            load_w4_scale_rows(r)
+        load_words(tab_win[1], tab_words[1])
+        gather_tab2_scales()
         gather_tab_scales()
         for q in range(4):
             move_tab_scale_rows(q)
-        load_words(tab_win[1], tab_words[1])
         load_words(tab_win[2], tab_words[2])
-        load_w1(0, 1)
-        load_w1(1, 1)
-        load_w1(2, 1)
-        load_words(tab2_win[0], tab2_words[0])
-        load_words(tab2_win[1], tab2_words[1])
-        permute_w4_words(0)
-        permute_w4_words(1)
-        gather_tab2_scales()
+        load_w1(1, 0)
+        nc.sync.dma_start(rows[R0 + NT : P, :], bval.rearrange("(c p) -> c p", p=P))
         for q in range(4):
             move_tab2_scale_rows(q)
-        cast_w1(on_scalar, 0, 0, 0, 4)
-        quantize_w1(0, 0, 0, 4)
+        load_w1(2, 0)
+        for a in range(KA):
+            load_w1(a, 1)
+        for b in range(HB):
+            load_words(tab2_win[b], tab2_words[b])
+
+        phase0 = [bank(t, "phase0%d" % t) for t in range(4)]
+        amp0 = [bank(4 + t, "amp0%d" % t) for t in range(4)]
+        gather_tab_words(0)
+        permute_w4_words(0)
+        cast_w1(on_scalar, 0, 0, 0, P)
+        quantize_w1(0, 0)
         permute_w4_scales(0)
+        phase_passes(phase0, 0, 0)
+        amp_wide(amp0, 0, 0)
+        gather_tab_words(1)
+        amp_wide(amp0, 1, 0)
+        gather_tab_words(2)
+        amp_wide(amp0, 2, 0)
+        cast_w1(on_vector, 1, 0, 0, P)
+        quantize_w1(1, 0)
+        phase_passes(phase0, 1, 0)
+        permute_w4_words(1)
         permute_w4_scales(1)
+        amp0_sb = sb("amp0_sb", [P, 4, S], F32, tag="w1_raw00")
+        for t in range(4):
+            nc.scalar.copy(amp0_sb[:, t, :], amp0[t][:])
         turned = bank(7, "turned")
         nc.tensor.transpose(turned[:, 0:P], rows[:], ident[:])
-        nc.scalar.copy(cols[:], turned[:, 0 : 2 * NT])
-        cast_w1(on_scalar, 1, 0, 0, 4)
-        gather_tab_words(0)
-        phase[0] = [bank(t, "phase0%d" % t) for t in range(4)]
-        phase_passes(phase[0], 0, 0)
-        quantize_w1(1, 0, 0, 4)
-        cast_w1(on_scalar, 2, 0, 0, 4)
-        gather_tab_words(1)
-        phase_passes(phase[0], 1, 0)
-        quantize_w1(2, 0, 0, 4)
-        gather_tab_words(2)
-        phase_passes(phase[0], 2, 0)
-        cast_w1(on_vector, 0, 1, 0, 4)
-        sines(phase[0], 0, 0)
-        sines(phase[0], 0, 1)
-        amp[0, 0] = bank(4, "amp00")
-        amp_bank(amp[0, 0], 0, 0)
-        amp[0, 1] = bank(5, "amp01")
-        amp_bank(amp[0, 1], 0, 1)
-        amp[0, 2] = bank(6, "amp02")
-        amp_bank(amp[0, 2], 0, 2)
-        amp[0, 3] = bank(7, "amp03")
-        amp_bank(amp[0, 3], 0, 3)
-        product(amp[0, 0], 0, 0)
-        quantize_w1(0, 1, 0, 4)
-        product(amp[0, 1], 0, 1)
-        cast_w1(on_vector, 1, 1, 2, 4)
-        cast_w1(on_scalar, 1, 1, 0, 2)
-        product(amp[0, 2], 0, 2)
-        product(amp[0, 3], 0, 3)
-        cast_w1(on_scalar, 2, 1, 0, 2)
-        cast_w1(on_vector, 2, 1, 2, 4)
-        quantize_w1(1, 1, 0, 4)
-        quantize_w1(2, 1, 2, 4)
-        quantize_w1(2, 1, 0, 2)
-        phase[1] = [bank(t, "phase1%d" % t) for t in range(4)]
-        phase_passes(phase[1], 0, 1)
-        amp[1, 0] = bank(4, "amp10")
-        amp_bank(amp[1, 0], 1, 0)
-        amp[1, 1] = bank(5, "amp11")
-        amp_bank(amp[1, 1], 1, 1)
-        phase_passes(phase[1], 1, 1)
-        phase_passes(phase[1], 2, 1)
-        amp[1, 2] = bank(6, "amp12")
-        amp_bank(amp[1, 2], 1, 2)
-        amp[1, 3] = bank(7, "amp13")
-        amp_bank(amp[1, 3], 1, 3)
-        quantize_h(0, 0, 2)
-        sines(phase[1], 1, 0)
-        sines(phase[1], 1, 1)
-        gather_tab2_words(0, 0)
-        product(amp[1, 0], 1, 0)
-        product(amp[1, 1], 1, 1)
-        product(amp[1, 2], 1, 2)
-        product(amp[1, 3], 1, 3)
-        quantize_h(1, 0, 1)
-        quantize_h(1, 1, 2)
-        acc[0] = bank(4 + 0, "acc0")
-        out_pass(acc[0], 0, 0)
-        acc[1] = bank(5 + 0, "acc1")
-        out_pass(acc[1], 0, 1)
-        acc[2] = bank(6 + 0, "acc2")
-        out_pass(acc[2], 0, 2)
-        acc[3] = bank(7 + 0, "acc3")
-        out_pass(acc[3], 0, 3)
-        gather_tab2_words(1, 0)
-        out_pass(acc[0], 1, 0)
-        out_pass(acc[1], 1, 1)
-        out_pass(acc[2], 1, 2)
-        out_pass(acc[3], 1, 3)
-        finish(0, False)
-        finish(1, False)
-        gather_tab2_words(0, 1)
-        acc[4] = bank(0 + 0, "acc4")
-        out_pass(acc[4], 0, 4)
-        acc[5] = bank(1 + 0, "acc5")
-        out_pass(acc[5], 0, 5)
-        acc[6] = bank(2 + 0, "acc6")
-        out_pass(acc[6], 0, 6)
-        acc[7] = bank(3 + 0, "acc7")
-        out_pass(acc[7], 0, 7)
-        gather_tab2_words(1, 1)
-        out_pass(acc[4], 1, 4)
-        out_pass(acc[5], 1, 5)
-        out_pass(acc[6], 1, 6)
-        out_pass(acc[7], 1, 7)
-        finish(2, False)
-        finish(3, False)
-        finish(4, False)
-        finish(5, True)
-        finish(6, False)
-        finish(7, True)
+        nc.scalar.copy(cols[:], turned[:, R0:P])
+        cast_w1(on_vector, 2, 0, 0, P)
+        quantize_w1(2, 0)
+        phase_passes(phase0, 2, 0)
+        amp1 = [bank(4 + jc, "amp1%d" % jc) for jc in range(2)]
+        for jc in range(2):
+            amp_bank(amp1[jc], 1, jc)
+        sines(phase0, 0, 0)
+        sines(phase0, 0, 1)
+
+        phase1 = [bank(n, "phase1%d" % n) for n in (6, 7, 2, 3)]
+        cast_w1(on_vector, 0, 1, 0, P)
+        quantize_w1(0, 1)
+        phase_passes(phase1, 0, 1)
+        amp1 = amp1 + [bank(jc, "amp1%d" % (2 + jc)) for jc in range(2)]
+        cast_w1(on_vector, 1, 1, 0, 64)
+        cast_w1(on_scalar, 1, 1, 64, P)
+        quantize_w1(1, 1)
+        phase_passes(phase1, 1, 1)
+        h0a = sb("h0a", [P, 2 * S], BF16, tag="w1_bf01")
+        product(h0a[:], amp0_sb[:, :, 0:256], 0, 0, 256)
+        cast_w1(on_vector, 2, 1, 0, 64)
+        cast_w1(on_scalar, 2, 1, 64, P)
+        quantize_w1(2, 1)
+        phase_passes(phase1, 2, 1)
+        for jc in range(2, 4):
+            amp_bank(amp1[jc], 1, jc)
+        h0b = sb("h0b", [P, 2 * S], BF16, tag="w1_bf21")
+        product(h0b[:], amp0_sb[:, :, 256:S], 0, 256, S)
+        quantize_h(h0a[:], 0, 0, 256)
+        quantize_h(h0b[:], 0, 256, S)
+        sines(phase1, 1, 0)
+        sines(phase1, 1, 1)
+        h1 = sb("h1", [P, 4 * S], BF16)
+        for jc in range(4):
+            product_bank(h1[:, jc * PASS : (jc + 1) * PASS], amp1[jc], 1, jc)
+            if jc % 2:
+                quantize_h(h1[:, (jc - 1) * PASS : (jc + 1) * PASS], 1, (jc - 1) * P, (jc + 1) * P)
+
+        acc = [bank(n, "acc%d" % n) for n in (6, 7, 2, 3, 4, 5, 0, 1)]
+        for b in range(HB):
+            for half in range(2):
+                gather_tab2_words(b, half)
+                for c in range(4 * half, 4 * half + 4):
+                    out_pass(acc[c], b, c)
+        for c in range(NT):
+            finish(acc[c], c, c in (4, 5, 7))

@@ -61,7 +61,7 @@ def tile_list_mesh_deeponet_sine_kernel(
         v_w = [sb("v_w%d" % a, [P, S], U32) for a in range(KA)]
         v_sg = sb("v_sg", [P, S], U8)
         v_s = sb("v_s", [P, KA, S // 4], I32)
-        v2_w = [sb("v2_w%d" % b, [P, S2], U32) for b in range(HB)]
+        v2_w = {}
         v2_sg = sb("v2_sg", [P, S2], U8)
         v2_s = sb("v2_s", [P, HB, S2 // 4], I32)
         w4_w = [sb("w4_w%d" % b, [P, KA, 2 * PASS], U8) for b in range(HB)]
@@ -114,9 +114,10 @@ def tile_list_mesh_deeponet_sine_kernel(
         def gather_tab2_scales():
             nc.vector.tensor_copy(v2_sg[:], tab2s_win[:].bitcast(U8).indirect(offs2_t[:]))
 
-        def gather_tab2_words(b, half):
+        def gather_tab2_words(b, half, tag):
+            v2_w[b, half] = sb("v2_w%d%d" % (b, half), [P, PASS], U32, tag=tag)
             nc.vector.tensor_copy(
-                v2_w[b][:, half * 512 : (half + 1) * 512],
+                v2_w[b, half][:],
                 tab2_win[b][:].bitcast(U32).indirect(offs2_t[:, half * 32 : (half + 1) * 32]),
             )
 
@@ -163,8 +164,8 @@ def tile_list_mesh_deeponet_sine_kernel(
                 for a in range(KA):
                     amp_pass(acc[:, t * P : (t + 1) * P], a, b, t, slice(jc * P, (jc + 1) * P))
 
-        def sines(acc, b, half):
-            j = slice(half * 256, (half + 1) * 256)
+        def sines(acc, b, j0, j1):
+            j = slice(j0, j1)
             for t in range(4):
                 nc.scalar.activation(sine[b][:, t, j], acc[t][:, j], ACT.Sin, bias=bias[:, b, t : t + 1])
 
@@ -182,16 +183,17 @@ def tile_list_mesh_deeponet_sine_kernel(
         def quantize_h(src, b, j0, j1):
             nc.vector.quantize_mx(h_w[b][:, j0:j1].bitcast(FP8X4), h_s[b][:, j0:j1], src)
 
-        def out_pass(acc, b, c):
+        def out_pass(acc, b, c, first):
             m = slice(c * P, (c + 1) * P)
+            half, ch = divmod(c, 4)
             nc.tensor.matmul_mx(
                 acc[:],
-                lhsT=v2_w[b][:, m].bitcast(FP8X4),
+                lhsT=v2_w[b, half][:, ch * P : (ch + 1) * P].bitcast(FP8X4),
                 lhsT_scale=v2_s[4:P, b, :].bitcast(U8)[:, m],
                 rhs=h_w[b][:].bitcast(FP8X4),
                 rhs_scale=h_s[b][:],
-                start=(b == 0),
-                stop=(b == HB - 1),
+                start=first,
+                stop=not first,
             )
 
         on_scalar, on_vector = nc.scalar.copy, nc.vector.tensor_copy
@@ -228,14 +230,14 @@ def tile_list_mesh_deeponet_sine_kernel(
         load_words(tab_win[1], tab_words[1])
         gather_tab2_scales()
         gather_tab_scales()
-        for q in range(4):
+        for q in (0, 2, 1, 3):
             move_tab_scale_rows(q)
         load_words(tab_win[2], tab_words[2])
         load_w1(1, 0)
         nc.sync.dma_start(rows[R0 + NT : P, :], bval.rearrange("(c p) -> c p", p=P))
-        for q in range(4):
-            move_tab2_scale_rows(q)
         load_w1(2, 0)
+        for q in (0, 2, 1, 3):
+            move_tab2_scale_rows(q)
         for a in range(KA):
             load_w1(a, 1)
         for b in range(HB):
@@ -271,22 +273,22 @@ def tile_list_mesh_deeponet_sine_kernel(
         amp1 = [bank(4 + jc, "amp1%d" % jc) for jc in range(2)]
         for jc in range(2):
             amp_bank(amp1[jc], 1, jc)
-        sines(phase0, 0, 0)
-        sines(phase0, 0, 1)
+        sines(phase0, 0, 0, 256)
+        sines(phase0, 0, 256, S)
 
         phase1 = [bank(n, "phase1%d" % n) for n in (6, 7, 2, 3)]
         cast_w1(on_vector, 0, 1, 0, P)
         quantize_w1(0, 1)
         phase_passes(phase1, 0, 1)
         amp1 = amp1 + [bank(jc, "amp1%d" % (2 + jc)) for jc in range(2)]
-        cast_w1(on_vector, 1, 1, 0, 64)
-        cast_w1(on_scalar, 1, 1, 64, P)
+        cast_w1(on_vector, 1, 1, 0, 56)
+        cast_w1(on_scalar, 1, 1, 56, P)
         quantize_w1(1, 1)
         phase_passes(phase1, 1, 1)
         h0a = sb("h0a", [P, 2 * S], BF16, tag="w1_bf01")
         product(h0a[:], amp0_sb[:, :, 0:256], 0, 0, 256)
-        cast_w1(on_vector, 2, 1, 0, 64)
-        cast_w1(on_scalar, 2, 1, 64, P)
+        cast_w1(on_vector, 2, 1, 0, 80)
+        cast_w1(on_scalar, 2, 1, 80, P)
         quantize_w1(2, 1)
         phase_passes(phase1, 2, 1)
         for jc in range(2, 4):
@@ -295,19 +297,21 @@ def tile_list_mesh_deeponet_sine_kernel(
         product(h0b[:], amp0_sb[:, :, 256:S], 0, 256, S)
         quantize_h(h0a[:], 0, 0, 256)
         quantize_h(h0b[:], 0, 256, S)
-        sines(phase1, 1, 0)
-        sines(phase1, 1, 1)
+        sines(phase1, 1, 0, 256)
+        sines(phase1, 1, 256, S)
+        gather_tab2_words(0, 0, "v2_a")
         h1 = sb("h1", [P, 4 * S], BF16)
         for jc in range(4):
             product_bank(h1[:, jc * PASS : (jc + 1) * PASS], amp1[jc], 1, jc)
             if jc % 2:
                 quantize_h(h1[:, (jc - 1) * PASS : (jc + 1) * PASS], 1, (jc - 1) * P, (jc + 1) * P)
 
-        acc = [bank(n, "acc%d" % n) for n in (6, 7, 2, 3, 4, 5, 0, 1)]
-        for b in range(HB):
-            for half in range(2):
-                gather_tab2_words(b, half)
-                for c in range(4 * half, 4 * half + 4):
-                    out_pass(acc[c], b, c)
+        acc = [bank(n, "acc%d" % n) for n in (4, 5, 0, 1, 6, 7, 2, 3)]
+        steps = [(0, 0, "v2_a", True), (1, 0, "v2_b", False), (1, 1, "v2_c", True), (0, 1, "v2_b", False)]
+        for b, half, tag, first in steps:
+            if (b, half) not in v2_w:
+                gather_tab2_words(b, half, tag)
+            for c in range(4 * half, 4 * half + 4):
+                out_pass(acc[c], b, c, first)
         for c in range(NT):
-            finish(acc[c], c, c in (4, 5, 7))
+            finish(acc[c], c, c in (5, 7))

@@ -22,10 +22,14 @@ PASS = 512
 KA = K // PASS
 HB = H // PASS
 NT = S2 // P
-ROWS = 16
-TS0 = P - KA * ROWS
-T2S0 = P - HB * ROWS
-R0 = P - 2 * NT
+BLOCKS = PASS // 32
+HALF = S // 2
+TAB_ROW0 = P - KA * BLOCKS
+TAB2_ROW0 = P - HB * BLOCKS
+VEC_ROW0 = P - 2 * NT
+V2_PLANE = 4
+QUADRANTS = (0, 2, 1, 3)
+VECTOR_SHARE = 64
 
 
 def tile_list_mesh_deeponet_sine_kernel(
@@ -48,7 +52,6 @@ def tile_list_mesh_deeponet_sine_kernel(
         rows = sb("rows", [P, P], F32)
         ident = sb("ident", [P, P], F32)
         cols = sb("cols", [P, 2 * NT], F32)
-        warm = sb("warm", [P, 8], F32)
 
         tab_win = [sb("tab_win%d" % a, [P, T], I32) for a in range(KA)]
         tabs_win = sb("tabs_win", [P, T // 4], I32)
@@ -85,21 +88,22 @@ def tile_list_mesh_deeponet_sine_kernel(
             src = w4_scales.rearrange("a (q r) t -> r q a t", r=4)[r]
             nc.sync.dma_start(w4s_raw[r:P:32], src.bitcast(I32))
 
-        def move_tab_scale_rows(q):
-            first = TS0 + 4 * KA * q
-            nc.sync.dma_start(v_s[32 * q : 32 * q + 4], v_sg[first : first + 4 * KA].bitcast(I32))
+        def move_tab_scale_rows(quad):
+            first = TAB_ROW0 + 4 * KA * quad
+            nc.sync.dma_start(v_s[32 * quad : 32 * quad + 4], v_sg[first : first + 4 * KA].bitcast(I32))
 
-        def move_tab2_scale_rows(q):
-            first = T2S0 + 4 * HB * q
-            nc.sync.dma_start(v2_s[32 * q + 4 : 32 * q + 8], v2_sg[first : first + 4 * HB].bitcast(I32))
+        def move_tab2_scale_rows(quad):
+            first = TAB2_ROW0 + 4 * HB * quad
+            plane = 32 * quad + V2_PLANE
+            nc.sync.dma_start(v2_s[plane : plane + 4], v2_sg[first : first + 4 * HB].bitcast(I32))
 
-        def permute_w4_words(b):
+        def deal_w4_words(b):
             nc.vector.tensor_copy(
                 w4_w[b][:].bitcast(U16).rearrange("p a (t m) -> p t a m", t=4),
                 w4_raw[:, :, b * 256 : (b + 1) * 256].bitcast(U16).rearrange("p a (m t) -> p t a m", t=4),
             )
 
-        def permute_w4_scales(b):
+        def deal_w4_scales(b):
             nc.vector.tensor_copy(
                 w4_s[b][:].rearrange("p a (t m) -> p t a m", t=4),
                 w4s_raw[:, :, b * 128 : (b + 1) * 128].bitcast(U8).rearrange("p a (m t) -> p t a m", t=4),
@@ -114,11 +118,11 @@ def tile_list_mesh_deeponet_sine_kernel(
         def gather_tab2_scales():
             nc.vector.tensor_copy(v2_sg[:], tab2s_win[:].bitcast(U8).indirect(offs2_t[:]))
 
-        def gather_tab2_words(b, half, tag):
-            v2_w[b, half] = sb("v2_w%d%d" % (b, half), [P, PASS], U32, tag=tag)
+        def gather_tab2_words(b, part, tag=None):
+            v2_w[b, part] = sb("v2_w%d%d" % (b, part), [P, PASS], U32, tag=tag)
             nc.vector.tensor_copy(
-                v2_w[b, half][:],
-                tab2_win[b][:].bitcast(U32).indirect(offs2_t[:, half * 32 : (half + 1) * 32]),
+                v2_w[b, part][:],
+                tab2_win[b][:].bitcast(U32).indirect(offs2_t[:, part * 32 : (part + 1) * 32]),
             )
 
         def cast_w1(copy, a, b, m0, m1):
@@ -127,14 +131,18 @@ def tile_list_mesh_deeponet_sine_kernel(
                 w1_raw[a][b][:].rearrange("p j (m t) -> p m j t", t=4)[:, m0:m1],
             )
 
+        def cast_w1_shared(a, b):
+            cast_w1(nc.vector.tensor_copy, a, b, 0, VECTOR_SHARE)
+            cast_w1(nc.scalar.copy, a, b, VECTOR_SHARE, P)
+
         def quantize_w1(a, b):
             nc.vector.quantize_mx(w1_w[a][b][:].bitcast(FP8X4), w1_s[a][b][:], w1_bf[a][b][:])
 
-        def phase_passes(acc, a, b):
+        def phase_passes(banks, a, b):
             for t in range(4):
                 m = slice(t * P, (t + 1) * P)
                 nc.tensor.matmul_mx(
-                    acc[t][:],
+                    banks[t][:],
                     lhsT=w1_w[a][b][:, m].bitcast(FP8X4),
                     lhsT_scale=w1_s[a][b][:, m],
                     rhs=v_w[a][:].bitcast(FP8X4),
@@ -155,19 +163,20 @@ def tile_list_mesh_deeponet_sine_kernel(
                 stop=(a == KA - 1),
             )
 
-        def amp_wide(acc, a, b):
+        def amp_passes(banks, a, b):
             for t in range(4):
-                amp_pass(acc[t][:], a, b, t, slice(0, S))
+                amp_pass(banks[t][:], a, b, t, slice(0, S))
 
-        def amp_bank(acc, b, jc):
+        def amp_bank(dst, b, jc):
             for t in range(4):
                 for a in range(KA):
-                    amp_pass(acc[:, t * P : (t + 1) * P], a, b, t, slice(jc * P, (jc + 1) * P))
+                    amp_pass(dst[:, t * P : (t + 1) * P], a, b, t, slice(jc * P, (jc + 1) * P))
 
-        def sines(acc, b, j0, j1):
-            j = slice(j0, j1)
-            for t in range(4):
-                nc.scalar.activation(sine[b][:, t, j], acc[t][:, j], ACT.Sin, bias=bias[:, b, t : t + 1])
+        def sines(banks, b):
+            for j0 in (0, HALF):
+                j = slice(j0, j0 + HALF)
+                for t in range(4):
+                    nc.scalar.activation(sine[b][:, t, j], banks[t][:, j], ACT.Sin, bias=bias[:, b, t : t + 1])
 
         def product(dst, amp, b, j0, j1):
             nc.vector.tensor_tensor(
@@ -177,67 +186,61 @@ def tile_list_mesh_deeponet_sine_kernel(
                 ALU.mult,
             )
 
-        def product_bank(dst, acc, b, jc):
-            product(dst, acc[:].rearrange("p (t j) -> p t j", t=4), b, jc * P, (jc + 1) * P)
+        def quantize_h(src, b, j0):
+            j = slice(j0, j0 + HALF)
+            nc.vector.quantize_mx(h_w[b][:, j].bitcast(FP8X4), h_s[b][:, j], src)
 
-        def quantize_h(src, b, j0, j1):
-            nc.vector.quantize_mx(h_w[b][:, j0:j1].bitcast(FP8X4), h_s[b][:, j0:j1], src)
+        def out_passes(banks, b, part, first):
+            for n in range(4):
+                c = 4 * part + n
+                nc.tensor.matmul_mx(
+                    banks[c][:],
+                    lhsT=v2_w[b, part][:, n * P : (n + 1) * P].bitcast(FP8X4),
+                    lhsT_scale=v2_s[V2_PLANE:P, b, :].bitcast(U8)[:, c * P : (c + 1) * P],
+                    rhs=h_w[b][:].bitcast(FP8X4),
+                    rhs_scale=h_s[b][:],
+                    start=first,
+                    stop=not first,
+                )
 
-        def out_pass(acc, b, c, first):
-            m = slice(c * P, (c + 1) * P)
-            half, ch = divmod(c, 4)
-            nc.tensor.matmul_mx(
-                acc[:],
-                lhsT=v2_w[b, half][:, ch * P : (ch + 1) * P].bitcast(FP8X4),
-                lhsT_scale=v2_s[4:P, b, :].bitcast(U8)[:, m],
-                rhs=h_w[b][:].bitcast(FP8X4),
-                rhs_scale=h_s[b][:],
-                start=first,
-                stop=not first,
-            )
-
-        on_scalar, on_vector = nc.scalar.copy, nc.vector.tensor_copy
-
-        def finish(acc, c, vector):
+        def finish(acc, c, on_vector):
             scale, shift = cols[:, c : c + 1], cols[:, NT + c : NT + c + 1]
-            if vector:
+            if on_vector:
                 nc.vector.tensor_scalar(res[c][:], acc[:], scale, shift, ALU.mult, ALU.add)
             else:
                 nc.scalar.activation(res[c][:], acc[:], ACT.Identity, bias=shift, scale=scale)
             nc.sync.dma_start(out[c * P : (c + 1) * P, :], res[c][:])
 
-        nc.vector.memset(tab2s_win[0:T2S0], 0)
-        nc.vector.memset(tabs_win[0:TS0], 0)
+        nc.vector.memset(tab2s_win[0:TAB2_ROW0], 0)
+        nc.vector.memset(tabs_win[0:TAB_ROW0], 0)
         nc.vector.memset(v_s[:], 0)
-        nc.gpsimd.memset(warm[:], 0.0)
         nc.gpsimd.memset(w4s_raw[:], 0)
         nc.gpsimd.memset(v2_s[:], 0)
-        nc.gpsimd.memset(rows[0:R0], 0.0)
+        nc.gpsimd.memset(rows[0:VEC_ROW0], 0.0)
         make_identity(nc, ident[:])
-        nc.scalar.activation(warm[:, 4:5], warm[:, 0:1], ACT.Sin)
 
         nc.sync.dma_start(offs2_t[:], offs2)
-        nc.sync.dma_start(tab2s_win[T2S0:P], tab2_scales.rearrange("b q t -> q b t").bitcast(I32))
+        nc.sync.dma_start(tab2s_win[TAB2_ROW0:P], tab2_scales.rearrange("b q t -> q b t").bitcast(I32))
         load_w1(0, 0)
         nc.sync.dma_start(offs_t[:], offs)
-        nc.sync.dma_start(tabs_win[TS0:P], tab_scales.rearrange("a q t -> q a t").bitcast(I32))
+        nc.sync.dma_start(tabs_win[TAB_ROW0:P], tab_scales.rearrange("a q t -> q a t").bitcast(I32))
         nc.sync.dma_start(w4_raw[:], w4_words.rearrange("a p n -> p a n").bitcast(I32))
         nc.sync.dma_start(bias[:], b1.rearrange("(b p t) -> p b t", b=HB, t=4))
-        nc.sync.dma_start(rows[R0 : R0 + NT, :], mask.rearrange("(c p) -> c p", p=P))
+        nc.sync.dma_start(rows[VEC_ROW0 : VEC_ROW0 + NT, :], mask.rearrange("(c p) -> c p", p=P))
         load_words(tab_win[0], tab_words[0])
         for r in range(4):
             load_w4_scale_rows(r)
         load_words(tab_win[1], tab_words[1])
         gather_tab2_scales()
         gather_tab_scales()
-        for q in (0, 2, 1, 3):
-            move_tab_scale_rows(q)
+        for quad in QUADRANTS:
+            move_tab_scale_rows(quad)
         load_words(tab_win[2], tab_words[2])
         load_w1(1, 0)
-        nc.sync.dma_start(rows[R0 + NT : P, :], bval.rearrange("(c p) -> c p", p=P))
+        nc.sync.dma_start(rows[VEC_ROW0 + NT : P, :], bval.rearrange("(c p) -> c p", p=P))
         load_w1(2, 0)
-        for q in (0, 2, 1, 3):
-            move_tab2_scale_rows(q)
+        for quad in QUADRANTS:
+            move_tab2_scale_rows(quad)
         for a in range(KA):
             load_w1(a, 1)
         for b in range(HB):
@@ -246,72 +249,71 @@ def tile_list_mesh_deeponet_sine_kernel(
         phase0 = [bank(t, "phase0%d" % t) for t in range(4)]
         amp0 = [bank(4 + t, "amp0%d" % t) for t in range(4)]
         gather_tab_words(0)
-        permute_w4_words(0)
-        cast_w1(on_scalar, 0, 0, 0, P)
+        deal_w4_words(0)
+        cast_w1(nc.scalar.copy, 0, 0, 0, P)
         quantize_w1(0, 0)
-        permute_w4_scales(0)
+        deal_w4_scales(0)
         phase_passes(phase0, 0, 0)
-        amp_wide(amp0, 0, 0)
+        amp_passes(amp0, 0, 0)
         gather_tab_words(1)
-        amp_wide(amp0, 1, 0)
+        amp_passes(amp0, 1, 0)
         gather_tab_words(2)
-        amp_wide(amp0, 2, 0)
-        cast_w1(on_vector, 1, 0, 0, P)
+        amp_passes(amp0, 2, 0)
+        cast_w1(nc.vector.tensor_copy, 1, 0, 0, P)
         quantize_w1(1, 0)
         phase_passes(phase0, 1, 0)
-        permute_w4_words(1)
-        permute_w4_scales(1)
+        deal_w4_words(1)
+        deal_w4_scales(1)
         amp0_sb = sb("amp0_sb", [P, 4, S], F32, tag="w1_raw00")
         for t in range(4):
             nc.scalar.copy(amp0_sb[:, t, :], amp0[t][:])
         turned = bank(7, "turned")
         nc.tensor.transpose(turned[:, 0:P], rows[:], ident[:])
-        nc.scalar.copy(cols[:], turned[:, R0:P])
-        cast_w1(on_vector, 2, 0, 0, P)
+        nc.scalar.copy(cols[:], turned[:, VEC_ROW0:P])
+        cast_w1(nc.vector.tensor_copy, 2, 0, 0, P)
         quantize_w1(2, 0)
         phase_passes(phase0, 2, 0)
         amp1 = [bank(4 + jc, "amp1%d" % jc) for jc in range(2)]
         for jc in range(2):
             amp_bank(amp1[jc], 1, jc)
-        sines(phase0, 0, 0, 256)
-        sines(phase0, 0, 256, S)
+        sines(phase0, 0)
 
         phase1 = [bank(n, "phase1%d" % n) for n in (6, 7, 2, 3)]
-        cast_w1(on_vector, 0, 1, 0, P)
+        cast_w1(nc.vector.tensor_copy, 0, 1, 0, P)
         quantize_w1(0, 1)
         phase_passes(phase1, 0, 1)
         amp1 = amp1 + [bank(jc, "amp1%d" % (2 + jc)) for jc in range(2)]
-        cast_w1(on_vector, 1, 1, 0, 56)
-        cast_w1(on_scalar, 1, 1, 56, P)
+        cast_w1_shared(1, 1)
         quantize_w1(1, 1)
         phase_passes(phase1, 1, 1)
-        h0a = sb("h0a", [P, 2 * S], BF16, tag="w1_bf01")
-        product(h0a[:], amp0_sb[:, :, 0:256], 0, 0, 256)
-        cast_w1(on_vector, 2, 1, 0, 80)
-        cast_w1(on_scalar, 2, 1, 80, P)
+        h0a = sb("h0a", [P, 4 * HALF], BF16, tag="w1_bf01")
+        product(h0a[:], amp0_sb[:, :, 0:HALF], 0, 0, HALF)
+        cast_w1_shared(2, 1)
         quantize_w1(2, 1)
         phase_passes(phase1, 2, 1)
         for jc in range(2, 4):
             amp_bank(amp1[jc], 1, jc)
-        h0b = sb("h0b", [P, 2 * S], BF16, tag="w1_bf21")
-        product(h0b[:], amp0_sb[:, :, 256:S], 0, 256, S)
-        quantize_h(h0a[:], 0, 0, 256)
-        quantize_h(h0b[:], 0, 256, S)
-        sines(phase1, 1, 0, 256)
-        sines(phase1, 1, 256, S)
-        gather_tab2_words(0, 0, "v2_a")
+        h0b = sb("h0b", [P, 4 * HALF], BF16, tag="w1_bf21")
+        quantize_h(h0a[:], 0, 0)
+        product(h0b[:], amp0_sb[:, :, HALF:S], 0, HALF, S)
+        quantize_h(h0b[:], 0, HALF)
+        sines(phase1, 1)
+        gather_tab2_words(0, 0)
         h1 = sb("h1", [P, 4 * S], BF16)
         for jc in range(4):
-            product_bank(h1[:, jc * PASS : (jc + 1) * PASS], amp1[jc], 1, jc)
-            if jc % 2:
-                quantize_h(h1[:, (jc - 1) * PASS : (jc + 1) * PASS], 1, (jc - 1) * P, (jc + 1) * P)
+            amp = amp1[jc][:].rearrange("p (t j) -> p t j", t=4)
+            product(h1[:, jc * PASS : (jc + 1) * PASS], amp, 1, jc * P, (jc + 1) * P)
+            if jc >= 2:
+                j0 = (jc - 2) * HALF
+                quantize_h(h1[:, 4 * j0 : 4 * (j0 + HALF)], 1, j0)
 
         acc = [bank(n, "acc%d" % n) for n in (4, 5, 0, 1, 6, 7, 2, 3)]
-        steps = [(0, 0, "v2_a", True), (1, 0, "v2_b", False), (1, 1, "v2_c", True), (0, 1, "v2_b", False)]
-        for b, half, tag, first in steps:
-            if (b, half) not in v2_w:
-                gather_tab2_words(b, half, tag)
-            for c in range(4 * half, 4 * half + 4):
-                out_pass(acc[c], b, c, first)
+        out_passes(acc, 0, 0, True)
+        gather_tab2_words(1, 0)
+        out_passes(acc, 1, 0, False)
+        gather_tab2_words(1, 1)
+        out_passes(acc, 1, 1, True)
+        gather_tab2_words(0, 1, tag="tab2_win1")
+        out_passes(acc, 0, 1, False)
         for c in range(NT):
-            finish(acc[c], c, c in (5, 7))
+            finish(acc[c], c, on_vector=(c >= 4 and c % 2 == 1))

@@ -95,7 +95,7 @@ def tile_list_mesh_deeponet_sine_kernel(
         def move_tab2_scale_rows(quad):
             first = TAB2_ROW0 + 4 * HB * quad
             plane = 32 * quad + V2_PLANE
-            nc.sync.dma_start(v2_s[plane : plane + 4], v2_sg[first : first + 4 * HB].bitcast(I32))
+            nc.gpsimd.dma_start(v2_s[plane : plane + 4], v2_sg[first : first + 4 * HB].bitcast(I32))
 
         def deal_w4_words(b):
             nc.vector.tensor_copy(

@@ -273,22 +273,27 @@ def tile_list_mesh_deeponet_sine_kernel(
         cast_w1(nc.vector.tensor_copy, 2, 0, 0, P)
         quantize_w1(2, 0)
         phase_passes(phase0, 2, 0)
-        amp1 = [bank(4 + jc, "amp1%d" % jc) for jc in range(2)]
-        for jc in range(2):
-            amp_bank(amp1[jc], 1, jc)
+        amp1_wide = [bank(4 + u, "amp1_wide%d" % u) for u in range(2)]
+        for u in range(2):
+            for t in (2 * u, 2 * u + 1):
+                for a in range(KA):
+                    amp_pass(amp1_wide[u][:, (t % 2) * HALF : (t % 2 + 1) * HALF], a, 1, t, slice(0, HALF))
         sines(phase0, 0)
 
         phase1 = [bank(n, "phase1%d" % n) for n in (6, 7, 2, 3)]
         cast_w1(nc.vector.tensor_copy, 0, 1, 0, P)
         quantize_w1(0, 1)
         phase_passes(phase1, 0, 1)
-        amp1 = amp1 + [bank(jc, "amp1%d" % (2 + jc)) for jc in range(2)]
+        amp1 = {2 + jc: bank(jc, "amp1%d" % (2 + jc)) for jc in range(2)}
         cast_w1_shared(1, 1)
         quantize_w1(1, 1)
         phase_passes(phase1, 1, 1)
         h0a = sb("h0a", [P, 4 * HALF], BF16, tag="w1_bf01")
         product(h0a[:], amp0_sb[:, :, 0:HALF], 0, 0, HALF)
         cast_w1_shared(2, 1)
+        amp1_sb = sb("amp1_sb", [P, 4, HALF], F32, tag="w1_raw21")
+        for u in range(2):
+            nc.scalar.copy(amp1_sb[:, 2 * u : 2 * u + 2, :].rearrange("p t j -> p (t j)"), amp1_wide[u][:])
         quantize_w1(2, 1)
         phase_passes(phase1, 2, 1)
         for jc in range(2, 4):
@@ -300,12 +305,12 @@ def tile_list_mesh_deeponet_sine_kernel(
         sines(phase1, 1)
         gather_tab2_words(0, 0)
         h1 = sb("h1", [P, 4 * S], BF16)
-        for jc in range(4):
+        product(h1[:, 0 : 4 * HALF], amp1_sb[:], 1, 0, HALF)
+        for jc in range(2, 4):
             amp = amp1[jc][:].rearrange("p (t j) -> p t j", t=4)
             product(h1[:, jc * PASS : (jc + 1) * PASS], amp, 1, jc * P, (jc + 1) * P)
-            if jc >= 2:
-                j0 = (jc - 2) * HALF
-                quantize_h(h1[:, 4 * j0 : 4 * (j0 + HALF)], 1, j0)
+            j0 = (jc - 2) * HALF
+            quantize_h(h1[:, 4 * j0 : 4 * (j0 + HALF)], 1, j0)
 
         acc = [bank(n, "acc%d" % n) for n in (4, 5, 0, 1, 6, 7, 2, 3)]
         out_passes(acc, 0, 0, True)

@@ -25,7 +25,7 @@ NT = S2 // P
 BLOCKS = PASS // 32
 HALF = S // 2
 TAB_ROW0 = P - KA * BLOCKS
-TAB2_ROW0 = P - HB * BLOCKS
+TAB2_ROW0 = P // 2 - BLOCKS
 VEC_ROW0 = P - 2 * NT
 V2_PLANE = 4
 QUADRANTS = (0, 2, 1, 3)
@@ -92,10 +92,11 @@ def tile_list_mesh_deeponet_sine_kernel(
             first = TAB_ROW0 + 4 * KA * quad
             nc.sync.dma_start(v_s[32 * quad : 32 * quad + 4], v_sg[first : first + 4 * KA].bitcast(I32))
 
-        def move_tab2_scale_rows(quad):
-            first = TAB2_ROW0 + 4 * HB * quad
-            plane = 32 * quad + V2_PLANE
-            nc.gpsimd.dma_start(v2_s[plane : plane + 4], v2_sg[first : first + 4 * HB].bitcast(I32))
+        def move_tab2_scale_rows(b, r):
+            first = 64 * b + TAB2_ROW0
+            nc.gpsimd.dma_start(
+                v2_s[V2_PLANE + r : P : 32, b, :], v2_sg[first + r : first + BLOCKS : 4].bitcast(I32)
+            )
 
         def deal_w4_words(b):
             nc.vector.tensor_copy(
@@ -190,42 +191,42 @@ def tile_list_mesh_deeponet_sine_kernel(
             j = slice(j0, j0 + HALF)
             nc.vector.quantize_mx(h_w[b][:, j].bitcast(FP8X4), h_s[b][:, j], src)
 
-        def out_passes(banks, b, part, first):
-            for n in range(4):
-                c = 4 * part + n
-                nc.tensor.matmul_mx(
-                    banks[c][:],
-                    lhsT=v2_w[b, part][:, n * P : (n + 1) * P].bitcast(FP8X4),
-                    lhsT_scale=v2_s[V2_PLANE:P, b, :].bitcast(U8)[:, c * P : (c + 1) * P],
-                    rhs=h_w[b][:].bitcast(FP8X4),
-                    rhs_scale=h_s[b][:],
-                    start=first,
-                    stop=not first,
-                )
+        def out_pass(dst, b, c, j, first):
+            n = c % 4
+            nc.tensor.matmul_mx(
+                dst,
+                lhsT=v2_w[b, c // 4][:, n * P : (n + 1) * P].bitcast(FP8X4),
+                lhsT_scale=v2_s[V2_PLANE:P, b, :].bitcast(U8)[:, c * P : (c + 1) * P],
+                rhs=h_w[b][:, j].bitcast(FP8X4),
+                rhs_scale=h_s[b][:, j],
+                start=first,
+                stop=not first,
+            )
 
-        def finish(acc, c, on_vector):
+        def finish(dst, acc, c, on_vector):
             scale, shift = cols[:, c : c + 1], cols[:, NT + c : NT + c + 1]
             if on_vector:
-                nc.vector.tensor_scalar(res[c][:], acc[:], scale, shift, ALU.mult, ALU.add)
+                nc.vector.tensor_scalar(dst, acc, scale, shift, ALU.mult, ALU.add)
             else:
-                nc.scalar.activation(res[c][:], acc[:], ACT.Identity, bias=shift, scale=scale)
-            nc.sync.dma_start(out[c * P : (c + 1) * P, :], res[c][:])
+                nc.scalar.activation(dst, acc, ACT.Identity, bias=shift, scale=scale)
 
-        nc.vector.memset(tab2s_win[0:TAB2_ROW0], 0)
+        for b in range(HB):
+            nc.vector.memset(tab2s_win[64 * b : 64 * b + TAB2_ROW0], 0)
         nc.vector.memset(tabs_win[0:TAB_ROW0], 0)
         nc.vector.memset(v_s[:], 0)
         nc.gpsimd.memset(w4s_raw[:], 0)
+        nc.gpsimd.dma_start(bias[:], b1.rearrange("(b p t) -> p b t", b=HB, t=4))
         nc.gpsimd.memset(v2_s[:], 0)
         nc.gpsimd.memset(rows[0:VEC_ROW0], 0.0)
         make_identity(nc, ident[:])
 
         nc.sync.dma_start(offs2_t[:], offs2)
-        nc.sync.dma_start(tab2s_win[TAB2_ROW0:P], tab2_scales.rearrange("b q t -> q b t").bitcast(I32))
+        for b in range(HB):
+            nc.sync.dma_start(tab2s_win[64 * b + TAB2_ROW0 : 64 * (b + 1)], tab2_scales[b].bitcast(I32))
         load_w1(0, 0)
         nc.sync.dma_start(offs_t[:], offs)
         nc.sync.dma_start(tabs_win[TAB_ROW0:P], tab_scales.rearrange("a q t -> q a t").bitcast(I32))
         nc.sync.dma_start(w4_raw[:], w4_words.rearrange("a p n -> p a n").bitcast(I32))
-        nc.sync.dma_start(bias[:], b1.rearrange("(b p t) -> p b t", b=HB, t=4))
         nc.sync.dma_start(rows[VEC_ROW0 : VEC_ROW0 + NT, :], mask.rearrange("(c p) -> c p", p=P))
         load_words(tab_win[0], tab_words[0])
         for r in range(4):
@@ -239,8 +240,9 @@ def tile_list_mesh_deeponet_sine_kernel(
         load_w1(1, 0)
         nc.sync.dma_start(rows[VEC_ROW0 + NT : P, :], bval.rearrange("(c p) -> c p", p=P))
         load_w1(2, 0)
-        for quad in QUADRANTS:
-            move_tab2_scale_rows(quad)
+        for b in range(HB):
+            for r in range(4):
+                move_tab2_scale_rows(b, r)
         for a in range(KA):
             load_w1(a, 1)
         for b in range(HB):
@@ -312,13 +314,35 @@ def tile_list_mesh_deeponet_sine_kernel(
             j0 = (jc - 2) * HALF
             quantize_h(h1[:, 4 * j0 : 4 * (j0 + HALF)], 1, j0)
 
-        acc = [bank(n, "acc%d" % n) for n in (4, 5, 0, 1, 6, 7, 2, 3)]
-        out_passes(acc, 0, 0, True)
-        gather_tab2_words(1, 0)
-        out_passes(acc, 1, 0, False)
-        gather_tab2_words(1, 1)
-        out_passes(acc, 1, 1, True)
-        gather_tab2_words(0, 1, tag="tab2_win1")
-        out_passes(acc, 0, 1, False)
-        for c in range(NT):
-            finish(acc[c], c, on_vector=(c >= 4 and c % 2 == 1))
+        every = slice(0, S)
+        halves = (slice(0, HALF), slice(HALF, S))
+        lead = [bank(n, "lead%d" % n) for n in (4, 3)]
+        acc = {c: bank(n, "acc%d" % c) for c, n in ((1, 5), (2, 0), (3, 1))}
+        for b in range(HB):
+            if b == 1:
+                gather_tab2_words(1, 0)
+            for n in range(2):
+                out_pass(lead[n][:, 0:HALF], b, 0, halves[n], b == 0)
+            for c in range(1, 4):
+                out_pass(acc[c][:], b, c, every, b == 0)
+        for n in range(2):
+            finish(res[0][:, halves[n]], lead[n][:, 0:HALF], 0, False)
+            nc.sync.dma_start(out[0:P, halves[n]], res[0][:, halves[n]])
+        for c in range(1, 4):
+            finish(res[c][:], acc[c][:], c, False)
+            nc.sync.dma_start(out[c * P : (c + 1) * P, :], res[c][:])
+        lead = [bank(n, "second_lead%d" % n) for n in (6, 4)]
+        for c, n in ((5, 7), (6, 2), (7, 3)):
+            acc[c] = bank(n, "acc%d" % c)
+        for b in (1, 0):
+            gather_tab2_words(b, 1, tag=None if b == 1 else "tab2_win1")
+            for n in range(2):
+                out_pass(lead[n][:, 0:HALF], b, 4, halves[n], b == 1)
+            for c in range(5, NT):
+                out_pass(acc[c][:], b, c, every, b == 1)
+        for n in range(2):
+            finish(res[4][:, halves[n]], lead[n][:, 0:HALF], 4, n == 0)
+            nc.sync.dma_start(out[4 * P : 5 * P, halves[n]], res[4][:, halves[n]])
+        for c in range(5, NT):
+            finish(res[c][:], acc[c][:], c, c % 2 == 1)
+            nc.sync.dma_start(out[c * P : (c + 1) * P, :], res[c][:])

@@ -317,32 +317,30 @@ def tile_list_mesh_deeponet_sine_kernel(
         every = slice(0, S)
         halves = (slice(0, HALF), slice(HALF, S))
         lead = [bank(n, "lead%d" % n) for n in (4, 3)]
-        acc = {c: bank(n, "acc%d" % c) for c, n in ((1, 5), (2, 0), (3, 1))}
-        for b in range(HB):
-            if b == 1:
-                gather_tab2_words(1, 0)
-            for n in range(2):
-                out_pass(lead[n][:, 0:HALF], b, 0, halves[n], b == 0)
-            for c in range(1, 4):
-                out_pass(acc[c][:], b, c, every, b == 0)
+        acc = {c: bank(n, "acc%d" % c) for c, n in ((1, 5), (2, 0), (3, 1), (4, 6), (5, 7), (6, 2))}
+        for n in range(2):
+            out_pass(lead[n][:, 0:HALF], 0, 0, halves[n], True)
+        for c in range(1, 4):
+            out_pass(acc[c][:], 0, c, every, True)
+        gather_tab2_words(0, 1)
+        for c in range(4, NT - 1):
+            out_pass(acc[c][:], 0, c, every, True)
+        gather_tab2_words(1, 0, tag="tab2_win0")
+        for n in range(2):
+            out_pass(lead[n][:, 0:HALF], 1, 0, halves[n], False)
+        for c in range(1, 4):
+            out_pass(acc[c][:], 1, c, every, False)
         for n in range(2):
             finish(res[0][:, halves[n]], lead[n][:, 0:HALF], 0, False)
             nc.sync.dma_start(out[0:P, halves[n]], res[0][:, halves[n]])
         for c in range(1, 4):
             finish(res[c][:], acc[c][:], c, False)
             nc.sync.dma_start(out[c * P : (c + 1) * P, :], res[c][:])
-        lead = [bank(n, "second_lead%d" % n) for n in (6, 4)]
-        for c, n in ((5, 7), (6, 2), (7, 3)):
-            acc[c] = bank(n, "acc%d" % c)
-        for b in (1, 0):
-            gather_tab2_words(b, 1, tag=None if b == 1 else "tab2_win1")
-            for n in range(2):
-                out_pass(lead[n][:, 0:HALF], b, 4, halves[n], b == 1)
-            for c in range(5, NT):
-                out_pass(acc[c][:], b, c, every, b == 1)
-        for n in range(2):
-            finish(res[4][:, halves[n]], lead[n][:, 0:HALF], 4, n == 0)
-            nc.sync.dma_start(out[4 * P : 5 * P, halves[n]], res[4][:, halves[n]])
-        for c in range(5, NT):
-            finish(res[c][:], acc[c][:], c, c % 2 == 1)
+        acc[NT - 1] = bank(4, "acc7")
+        out_pass(acc[NT - 1][:], 0, NT - 1, every, True)
+        gather_tab2_words(1, 1)
+        for c in range(4, NT):
+            out_pass(acc[c][:], 1, c, every, False)
+        for c in range(4, NT):
+            finish(res[c][:], acc[c][:], c, c < NT - 1)
             nc.sync.dma_start(out[c * P : (c + 1) * P, :], res[c][:])

@@ -25,7 +25,7 @@ NT = S2 // P
 BLOCKS = PASS // 32
 HALF = S // 2
 TAB_ROW0 = P - KA * BLOCKS
-TAB2_ROW0 = P // 2 - BLOCKS
+TAB2_ROW0 = P - HB * BLOCKS
 VEC_ROW0 = P - 2 * NT
 V2_PLANE = 4
 QUADRANTS = (0, 2, 1, 3)
@@ -51,7 +51,6 @@ def tile_list_mesh_deeponet_sine_kernel(
         bias = sb("bias", [P, HB, 4], F32)
         rows = sb("rows", [P, P], F32)
         ident = sb("ident", [P, P], F32)
-        cols = sb("cols", [P, 2 * NT], F32)
 
         tab_win = [sb("tab_win%d" % a, [P, T], I32) for a in range(KA)]
         tabs_win = sb("tabs_win", [P, T // 4], I32)
@@ -66,7 +65,6 @@ def tile_list_mesh_deeponet_sine_kernel(
         v_s = sb("v_s", [P, KA, S // 4], I32)
         v2_w = {}
         v2_sg = sb("v2_sg", [P, S2], U8)
-        v2_s = sb("v2_s", [P, HB, S2 // 4], I32)
         w4_w = [sb("w4_w%d" % b, [P, KA, 2 * PASS], U8) for b in range(HB)]
         w4_s = [sb("w4_s%d" % b, [P, KA, PASS], U8) for b in range(HB)]
         w1_bf = [[sb("w1_bf%d%d" % (a, b), [P, 4 * PASS], BF16) for b in range(HB)] for a in range(KA)]
@@ -92,11 +90,10 @@ def tile_list_mesh_deeponet_sine_kernel(
             first = TAB_ROW0 + 4 * KA * quad
             nc.sync.dma_start(v_s[32 * quad : 32 * quad + 4], v_sg[first : first + 4 * KA].bitcast(I32))
 
-        def move_tab2_scale_rows(b, r):
-            first = 64 * b + TAB2_ROW0
-            nc.gpsimd.dma_start(
-                v2_s[V2_PLANE + r : P : 32, b, :], v2_sg[first + r : first + BLOCKS : 4].bitcast(I32)
-            )
+        def move_tab2_scale_rows(quad):
+            first = TAB2_ROW0 + 4 * HB * quad
+            plane = 32 * quad + V2_PLANE
+            nc.gpsimd.dma_start(v2_s[plane : plane + 4], v2_sg[first : first + 4 * HB].bitcast(I32))
 
         def deal_w4_words(b):
             nc.vector.tensor_copy(
@@ -173,11 +170,10 @@ def tile_list_mesh_deeponet_sine_kernel(
                 for a in range(KA):
                     amp_pass(dst[:, t * P : (t + 1) * P], a, b, t, slice(jc * P, (jc + 1) * P))
 
-        def sines(banks, b):
-            for j0 in (0, HALF):
-                j = slice(j0, j0 + HALF)
-                for t in range(4):
-                    nc.scalar.activation(sine[b][:, t, j], banks[t][:, j], ACT.Sin, bias=bias[:, b, t : t + 1])
+        def sines(banks, b, j0):
+            j = slice(j0, j0 + HALF)
+            for t in range(4):
+                nc.scalar.activation(sine[b][:, t, j], banks[t][:, j], ACT.Sin, bias=bias[:, b, t : t + 1])
 
         def product(dst, amp, b, j0, j1):
             nc.vector.tensor_tensor(
@@ -210,39 +206,37 @@ def tile_list_mesh_deeponet_sine_kernel(
             else:
                 nc.scalar.activation(dst, acc, ACT.Identity, bias=shift, scale=scale)
 
-        for b in range(HB):
-            nc.vector.memset(tab2s_win[64 * b : 64 * b + TAB2_ROW0], 0)
+        nc.vector.memset(tab2s_win[0:TAB2_ROW0], 0)
         nc.vector.memset(tabs_win[0:TAB_ROW0], 0)
         nc.vector.memset(v_s[:], 0)
         nc.gpsimd.memset(w4s_raw[:], 0)
-        nc.gpsimd.dma_start(bias[:], b1.rearrange("(b p t) -> p b t", b=HB, t=4))
-        nc.gpsimd.memset(v2_s[:], 0)
         nc.gpsimd.memset(rows[0:VEC_ROW0], 0.0)
         make_identity(nc, ident[:])
 
         nc.sync.dma_start(offs2_t[:], offs2)
-        for b in range(HB):
-            nc.sync.dma_start(tab2s_win[64 * b + TAB2_ROW0 : 64 * (b + 1)], tab2_scales[b].bitcast(I32))
+        nc.sync.dma_start(tab2s_win[TAB2_ROW0:P], tab2_scales.rearrange("b q t -> q b t").bitcast(I32))
         load_w1(0, 0)
         nc.sync.dma_start(offs_t[:], offs)
         nc.sync.dma_start(tabs_win[TAB_ROW0:P], tab_scales.rearrange("a q t -> q a t").bitcast(I32))
         nc.sync.dma_start(w4_raw[:], w4_words.rearrange("a p n -> p a n").bitcast(I32))
+        nc.sync.dma_start(bias[:], b1.rearrange("(b p t) -> p b t", b=HB, t=4))
         nc.sync.dma_start(rows[VEC_ROW0 : VEC_ROW0 + NT, :], mask.rearrange("(c p) -> c p", p=P))
-        load_words(tab_win[0], tab_words[0])
         for r in range(4):
             load_w4_scale_rows(r)
+        load_words(tab_win[0], tab_words[0])
         load_words(tab_win[1], tab_words[1])
         gather_tab2_scales()
         gather_tab_scales()
+        v2_s = sb("v2_s", [P, HB, S2 // 4], I32, tag="tabs_win")
+        nc.gpsimd.memset(v2_s[:], 0)
         for quad in QUADRANTS:
             move_tab_scale_rows(quad)
         load_words(tab_win[2], tab_words[2])
         load_w1(1, 0)
         nc.sync.dma_start(rows[VEC_ROW0 + NT : P, :], bval.rearrange("(c p) -> c p", p=P))
         load_w1(2, 0)
-        for b in range(HB):
-            for r in range(4):
-                move_tab2_scale_rows(b, r)
+        for quad in QUADRANTS:
+            move_tab2_scale_rows(quad)
         for a in range(KA):
             load_w1(a, 1)
         for b in range(HB):
@@ -269,18 +263,20 @@ def tile_list_mesh_deeponet_sine_kernel(
         amp0_sb = sb("amp0_sb", [P, 4, S], F32, tag="w1_raw00")
         for t in range(4):
             nc.scalar.copy(amp0_sb[:, t, :], amp0[t][:])
-        turned = bank(7, "turned")
+        turned = bank(5, "turned")
         nc.tensor.transpose(turned[:, 0:P], rows[:], ident[:])
-        nc.scalar.copy(cols[:], turned[:, VEC_ROW0:P])
         cast_w1(nc.vector.tensor_copy, 2, 0, 0, P)
         quantize_w1(2, 0)
         phase_passes(phase0, 2, 0)
+        sines(phase0, 0, 0)
+        cols = sb("cols", [P, 2 * NT], F32, tag="w1_w20")
+        nc.scalar.copy(cols[:], turned[:, VEC_ROW0:P])
         amp1_wide = [bank(4 + u, "amp1_wide%d" % u) for u in range(2)]
         for u in range(2):
             for t in (2 * u, 2 * u + 1):
                 for a in range(KA):
                     amp_pass(amp1_wide[u][:, (t % 2) * HALF : (t % 2 + 1) * HALF], a, 1, t, slice(0, HALF))
-        sines(phase0, 0)
+        sines(phase0, 0, HALF)
 
         phase1 = [bank(n, "phase1%d" % n) for n in (6, 7, 2, 3)]
         cast_w1(nc.vector.tensor_copy, 0, 1, 0, P)
@@ -304,7 +300,8 @@ def tile_list_mesh_deeponet_sine_kernel(
         quantize_h(h0a[:], 0, 0)
         product(h0b[:], amp0_sb[:, :, HALF:S], 0, HALF, S)
         quantize_h(h0b[:], 0, HALF)
-        sines(phase1, 1)
+        sines(phase1, 1, 0)
+        sines(phase1, 1, HALF)
         gather_tab2_words(0, 0)
         h1 = sb("h1", [P, 4 * S], BF16)
         product(h1[:, 0 : 4 * HALF], amp1_sb[:], 1, 0, HALF)

@@ -22,14 +22,15 @@ PASS = 512
 KA = K // PASS
 HB = H // PASS
 NT = S2 // P
+NJ = S // P
 BLOCKS = PASS // 32
 HALF = S // 2
+PAIR = 2 * P
 TAB_ROW0 = P - KA * BLOCKS
 TAB2_ROW0 = P - HB * BLOCKS
 VEC_ROW0 = P - 2 * NT
 V2_PLANE = 4
 QUADRANTS = (0, 2, 1, 3)
-VECTOR_SHARE = 64
 
 
 def tile_list_mesh_deeponet_sine_kernel(
@@ -51,97 +52,116 @@ def tile_list_mesh_deeponet_sine_kernel(
         bias = sb("bias", [P, HB, 4], F32)
         rows = sb("rows", [P, P], F32)
         ident = sb("ident", [P, P], F32)
+        cols = sb("cols", [P, 2 * NT], F32)
 
         tab_win = [sb("tab_win%d" % a, [P, T], I32) for a in range(KA)]
         tabs_win = sb("tabs_win", [P, T // 4], I32)
         tab2_win = [sb("tab2_win%d" % b, [P, T2], I32) for b in range(HB)]
         tab2s_win = sb("tab2s_win", [P, T2 // 4], I32)
-        w4_raw = sb("w4_raw", [P, KA, H // 2], I32)
-        w4s_raw = sb("w4s_raw", [P, KA, H // 4], I32)
-        w1_raw = [[sb("w1_raw%d%d" % (a, b), [P, 4, PASS], F32) for b in range(HB)] for a in range(KA)]
+        w4_w = sb("w4_w", [P, KA, 2 * H], U8)
+        w4_s = sb("w4_s", [P, KA, H], U8)
+        w1_half = {(a, b): sb("w1_half%d%d" % (a, b), [P, 4, PASS], F32) for a in range(KA) for b in range(HB)}
 
         v_w = [sb("v_w%d" % a, [P, S], U32) for a in range(KA)]
         v_sg = sb("v_sg", [P, S], U8)
         v_s = sb("v_s", [P, KA, S // 4], I32)
         v2_w = {}
         v2_sg = sb("v2_sg", [P, S2], U8)
-        w4_w = [sb("w4_w%d" % b, [P, KA, 2 * PASS], U8) for b in range(HB)]
-        w4_s = [sb("w4_s%d" % b, [P, KA, PASS], U8) for b in range(HB)]
-        w1_bf = [[sb("w1_bf%d%d" % (a, b), [P, 4 * PASS], BF16) for b in range(HB)] for a in range(KA)]
-        w1_w = [[sb("w1_w%d%d" % (a, b), [P, PASS], U32) for b in range(HB)] for a in range(KA)]
+        w1_bf = {}
+        w1_w = {(a, b): sb("w1_w%d%d" % (a, b), [P, PASS], U32) for a in range(KA) for b in range(HB)}
         w1_s = [[sb("w1_s%d%d" % (a, b), [P, PASS], U8) for b in range(HB)] for a in range(KA)]
-        sine = [sb("sine%d" % b, [P, 4, S], F32) for b in range(HB)]
-        h_w = [sb("h_w%d" % b, [P, S], U32) for b in range(HB)]
+        amp_t = [[sb("amp_t%d%d" % (b, g), [P, PASS], F32) for g in range(NJ)] for b in range(HB)]
+        sine = [[sb("sine%d%d" % (b, u), [P, 4, HALF], F32) for u in range(2)] for b in range(HB)]
+        h_bf = {}
+        h_w = {}
         h_s = [sb("h_s%d" % b, [P, S], U8) for b in range(HB)]
-        res = [sb("res%d" % c, [P, S], F32) for c in range(NT)]
-
-        def load_w1(a, b):
-            src = w1[a * PASS : (a + 1) * PASS, b * PASS : (b + 1) * PASS]
-            nc.sync.dma_start(w1_raw[a][b][:], src.rearrange("(p j) c -> p j c", j=4))
 
         def load_words(win, words):
             nc.sync.dma_start(win[:], words.rearrange("p t i -> p (t i)").bitcast(I32))
 
+        def load_w1_half(a, b):
+            src = w1[a * PASS : (a + 1) * PASS, b * PASS : (b + 1) * PASS]
+            nc.sync.dma_start(w1_half[a, b][:], src.rearrange("(p j) c -> p j c", j=4))
+
         def load_w4_scale_rows(r):
             src = w4_scales.rearrange("a (q r) t -> r q a t", r=4)[r]
-            nc.sync.dma_start(w4s_raw[r:P:32], src.bitcast(I32))
+            nc.sync.dma_start(w4_s[r:P:32].bitcast(I32), src.bitcast(I32))
 
         def move_tab_scale_rows(quad):
-            first = TAB_ROW0 + 4 * KA * quad
-            nc.sync.dma_start(v_s[32 * quad : 32 * quad + 4], v_sg[first : first + 4 * KA].bitcast(I32))
+            first = TAB_ROW0 + BLOCKS + 8 * quad
+            nc.sync.dma_start(v_s[32 * quad : 32 * quad + 4, 0:2], v_sg[first : first + 8].bitcast(I32))
+
+        def move_last_tab_scale_rows(quad):
+            first = TAB_ROW0 + 4 * quad
+            nc.sync.dma_start(v_s[32 * quad : 32 * quad + 4, 2], v_sg[first : first + 4].bitcast(I32))
 
         def move_tab2_scale_rows(quad):
             first = TAB2_ROW0 + 4 * HB * quad
             plane = 32 * quad + V2_PLANE
             nc.gpsimd.dma_start(v2_s[plane : plane + 4], v2_sg[first : first + 4 * HB].bitcast(I32))
 
-        def deal_w4_words(b):
-            nc.vector.tensor_copy(
-                w4_w[b][:].bitcast(U16).rearrange("p a (t m) -> p t a m", t=4),
-                w4_raw[:, :, b * 256 : (b + 1) * 256].bitcast(U16).rearrange("p a (m t) -> p t a m", t=4),
-            )
-
-        def deal_w4_scales(b):
-            nc.vector.tensor_copy(
-                w4_s[b][:].rearrange("p a (t m) -> p t a m", t=4),
-                w4s_raw[:, :, b * 128 : (b + 1) * 128].bitcast(U8).rearrange("p a (m t) -> p t a m", t=4),
-            )
-
-        def gather_tab_scales():
-            nc.vector.tensor_copy(v_sg[:], tabs_win[:].bitcast(U8).indirect(offs_t[:]))
-
         def gather_tab_words(a):
             nc.vector.tensor_copy(v_w[a][:], tab_win[a][:].bitcast(U32).indirect(offs_t[:]))
 
-        def gather_tab2_scales():
-            nc.vector.tensor_copy(v2_sg[:], tab2s_win[:].bitcast(U8).indirect(offs2_t[:]))
+        def gather_tab2_words(b, c0, c1, tag=None):
+            tile = sb("v2_w%d%d" % (b, c0), [P, (c1 - c0) * P], U32, tag=tag)
+            for c in range(c0, c1):
+                v2_w[b, c] = tile[:, (c - c0) * P : (c - c0 + 1) * P]
+            nc.vector.tensor_copy(tile[:], tab2_win[b][:].bitcast(U32).indirect(offs2_t[:, c0 * 8 : c1 * 8]))
 
-        def gather_tab2_words(b, part, tag=None):
-            v2_w[b, part] = sb("v2_w%d%d" % (b, part), [P, PASS], U32, tag=tag)
-            nc.vector.tensor_copy(
-                v2_w[b, part][:],
-                tab2_win[b][:].bitcast(U32).indirect(offs2_t[:, part * 32 : (part + 1) * 32]),
-            )
-
-        def cast_w1(copy, a, b, m0, m1):
+        def cast_w1(copy, a, b, m0=0, m1=P, t0=0, t1=4):
+            if (a, b) not in w1_bf:
+                w1_bf[a, b] = sb("w1_bf%d%d" % (a, b), [P, 4 * PASS], BF16)
+            raw = w1_half[a, b][:]
             copy(
-                w1_bf[a][b][:].rearrange("p (t m j) -> p m j t", t=4, j=4)[:, m0:m1],
-                w1_raw[a][b][:].rearrange("p j (m t) -> p m j t", t=4)[:, m0:m1],
+                w1_bf[a, b][:].rearrange("p (t m j) -> p m j t", t=4, j=4)[:, m0:m1, :, t0:t1],
+                raw.rearrange("p j (m t) -> p m j t", t=4)[:, m0:m1, :, t0:t1],
             )
 
-        def cast_w1_shared(a, b):
-            cast_w1(nc.vector.tensor_copy, a, b, 0, VECTOR_SHARE)
-            cast_w1(nc.scalar.copy, a, b, VECTOR_SHARE, P)
+        def cast_shared(a, b, share):
+            cast_w1(nc.vector.tensor_copy, a, b, 0, share)
+            cast_w1(nc.scalar.copy, a, b, share, P)
 
-        def quantize_w1(a, b):
-            nc.vector.quantize_mx(w1_w[a][b][:].bitcast(FP8X4), w1_s[a][b][:], w1_bf[a][b][:])
+        def quantize_w1(a, b, t0=0, t1=4):
+            m = slice(t0 * P, t1 * P)
+            nc.vector.quantize_mx(
+                w1_w[a, b][:, m].bitcast(FP8X4), w1_s[a][b][:, m], w1_bf[a, b][:, 4 * t0 * P : 4 * t1 * P]
+            )
 
-        def phase_passes(banks, a, b):
+        def amp_passes(banks, a, b):
+            for g in range(NJ):
+                j = slice(g * P, (g + 1) * P)
+                nc.tensor.matmul_mx(
+                    banks[g][:],
+                    lhsT=v_w[a][:, j].bitcast(FP8X4),
+                    lhsT_scale=v_s[:, a, :].bitcast(U8)[:, j],
+                    rhs=w4_w[:, a, 2 * b * PASS : 2 * (b + 1) * PASS].bitcast(FP4X4),
+                    rhs_scale=w4_s[:, a, b * PASS : (b + 1) * PASS],
+                    start=(a == 0),
+                    stop=(a == KA - 1),
+                )
+
+        def park(banks, b, on_vector):
+            for g in range(NJ):
+                copy = nc.vector.tensor_copy if g in on_vector else nc.scalar.copy
+                copy(
+                    amp_t[b][g][:].rearrange("p (t m) -> p t m", t=4),
+                    banks[g][:].rearrange("p (m t) -> p t m", t=4),
+                )
+
+        def turn_amp(b, g):
+            dst = bank(g, "amp%d%d" % (b, g))
             for t in range(4):
+                m = slice(t * P, (t + 1) * P)
+                nc.tensor.transpose(dst[:, m], amp_t[b][g][:, m], ident[:])
+            return dst
+
+        def phase_passes(banks, a, b, t0=0, t1=4):
+            for t in range(t0, t1):
                 m = slice(t * P, (t + 1) * P)
                 nc.tensor.matmul_mx(
                     banks[t][:],
-                    lhsT=w1_w[a][b][:, m].bitcast(FP8X4),
+                    lhsT=w1_w[a, b][:, m].bitcast(FP8X4),
                     lhsT_scale=w1_s[a][b][:, m],
                     rhs=v_w[a][:].bitcast(FP8X4),
                     rhs_scale=v_s[:, a, :].bitcast(U8),
@@ -149,49 +169,33 @@ def tile_list_mesh_deeponet_sine_kernel(
                     stop=(a == KA - 1),
                 )
 
-        def amp_pass(dst, a, b, t, j):
-            c0 = t * P
-            nc.tensor.matmul_mx(
-                dst,
-                lhsT=w4_w[b][:, a, 2 * c0 : 2 * (c0 + P)].bitcast(FP4X4),
-                lhsT_scale=w4_s[b][:, a, c0 : c0 + P],
-                rhs=v_w[a][:, j].bitcast(FP8X4),
-                rhs_scale=v_s[:, a, :].bitcast(U8)[:, j],
-                start=(a == 0),
-                stop=(a == KA - 1),
-            )
+        def sines(banks, b):
+            for u in range(2):
+                j = slice(u * HALF, (u + 1) * HALF)
+                for t in range(4):
+                    nc.scalar.activation(sine[b][u][:, t, :], banks[t][:, j], ACT.Sin, bias=bias[:, b, t : t + 1])
 
-        def amp_passes(banks, a, b):
-            for t in range(4):
-                amp_pass(banks[t][:], a, b, t, slice(0, S))
-
-        def amp_bank(dst, b, jc):
-            for t in range(4):
-                for a in range(KA):
-                    amp_pass(dst[:, t * P : (t + 1) * P], a, b, t, slice(jc * P, (jc + 1) * P))
-
-        def sines(banks, b, j0):
-            j = slice(j0, j0 + HALF)
-            for t in range(4):
-                nc.scalar.activation(sine[b][:, t, j], banks[t][:, j], ACT.Sin, bias=bias[:, b, t : t + 1])
-
-        def product(dst, amp, b, j0, j1):
+        def product(amp, b, g, tag=None):
+            u, n = divmod(g, 2)
+            if n == 0:
+                h_bf[b, u] = sb("h_bf%d%d" % (b, u), [P, 4 * HALF], BF16, tag=tag)
             nc.vector.tensor_tensor(
-                dst.rearrange("p (c i t) -> p c t i", i=4, t=4),
-                amp.rearrange("p t (c i) -> p c t i", i=4),
-                sine[b][:, :, j0:j1].rearrange("p t (c i) -> p c t i", i=4),
+                h_bf[b, u][:, n * PASS : (n + 1) * PASS].rearrange("p (c i t) -> p c t i", i=4, t=4),
+                amp[:].rearrange("p (t c i) -> p c t i", t=4, i=4),
+                sine[b][u][:, :, n * P : (n + 1) * P].rearrange("p t (c i) -> p c t i", i=4),
                 ALU.mult,
             )
 
-        def quantize_h(src, b, j0):
-            j = slice(j0, j0 + HALF)
-            nc.vector.quantize_mx(h_w[b][:, j].bitcast(FP8X4), h_s[b][:, j], src)
+        def quantize_h(b, u, tag=None):
+            if u == 0:
+                h_w[b] = sb("h_w%d" % b, [P, S], U32, tag=tag)
+            j = slice(u * HALF, (u + 1) * HALF)
+            nc.vector.quantize_mx(h_w[b][:, j].bitcast(FP8X4), h_s[b][:, j], h_bf[b, u][:])
 
         def out_pass(dst, b, c, j, first):
-            n = c % 4
             nc.tensor.matmul_mx(
                 dst,
-                lhsT=v2_w[b, c // 4][:, n * P : (n + 1) * P].bitcast(FP8X4),
+                lhsT=v2_w[b, c].bitcast(FP8X4),
                 lhsT_scale=v2_s[V2_PLANE:P, b, :].bitcast(U8)[:, c * P : (c + 1) * P],
                 rhs=h_w[b][:, j].bitcast(FP8X4),
                 rhs_scale=h_s[b][:, j],
@@ -206,138 +210,129 @@ def tile_list_mesh_deeponet_sine_kernel(
             else:
                 nc.scalar.activation(dst, acc, ACT.Identity, bias=shift, scale=scale)
 
-        nc.vector.memset(tab2s_win[0:TAB2_ROW0], 0)
         nc.vector.memset(tabs_win[0:TAB_ROW0], 0)
         nc.vector.memset(v_s[:], 0)
-        nc.gpsimd.memset(w4s_raw[:], 0)
+        nc.vector.memset(tab2s_win[0:TAB2_ROW0], 0)
+        nc.gpsimd.memset(w4_s[:].bitcast(I32), 0)
         nc.gpsimd.memset(rows[0:VEC_ROW0], 0.0)
         make_identity(nc, ident[:])
 
-        nc.sync.dma_start(offs2_t[:], offs2)
-        nc.sync.dma_start(tab2s_win[TAB2_ROW0:P], tab2_scales.rearrange("b q t -> q b t").bitcast(I32))
-        load_w1(0, 0)
         nc.sync.dma_start(offs_t[:], offs)
-        nc.sync.dma_start(tabs_win[TAB_ROW0:P], tab_scales.rearrange("a q t -> q a t").bitcast(I32))
-        nc.sync.dma_start(w4_raw[:], w4_words.rearrange("a p n -> p a n").bitcast(I32))
-        nc.sync.dma_start(bias[:], b1.rearrange("(b p t) -> p b t", b=HB, t=4))
-        nc.sync.dma_start(rows[VEC_ROW0 : VEC_ROW0 + NT, :], mask.rearrange("(c p) -> c p", p=P))
+        nc.sync.dma_start(tabs_win[TAB_ROW0 + BLOCKS : P], tab_scales[0:2].rearrange("a q t -> q a t").bitcast(I32))
+        nc.sync.dma_start(tabs_win[TAB_ROW0 : TAB_ROW0 + BLOCKS], tab_scales[2].bitcast(I32))
+        nc.sync.dma_start(w4_w[:].bitcast(I32), w4_words.rearrange("a p n -> p a n").bitcast(I32))
         for r in range(4):
             load_w4_scale_rows(r)
         load_words(tab_win[0], tab_words[0])
+        nc.sync.dma_start(offs2_t[:], offs2)
+        nc.sync.dma_start(tab2s_win[TAB2_ROW0:P], tab2_scales.rearrange("b q t -> q b t").bitcast(I32))
         load_words(tab_win[1], tab_words[1])
-        gather_tab2_scales()
-        gather_tab_scales()
+        nc.vector.tensor_copy(v_sg[:], tabs_win[:].bitcast(U8).indirect(offs_t[:]))
         v2_s = sb("v2_s", [P, HB, S2 // 4], I32, tag="tabs_win")
-        nc.gpsimd.memset(v2_s[:], 0)
         for quad in QUADRANTS:
             move_tab_scale_rows(quad)
+        nc.gpsimd.memset(v2_s[:], 0)
         load_words(tab_win[2], tab_words[2])
-        load_w1(1, 0)
+        load_w1_half(0, 0)
+        for quad in QUADRANTS:
+            move_last_tab_scale_rows(quad)
+        load_w1_half(1, 0)
+        load_w1_half(2, 0)
+        nc.sync.dma_start(rows[VEC_ROW0 : VEC_ROW0 + NT, :], mask.rearrange("(c p) -> c p", p=P))
         nc.sync.dma_start(rows[VEC_ROW0 + NT : P, :], bval.rearrange("(c p) -> c p", p=P))
-        load_w1(2, 0)
+        nc.sync.dma_start(bias[:], b1.rearrange("(b p t) -> p b t", b=HB, t=4))
+        for a in range(KA):
+            gather_tab_words(a)
+        nc.vector.tensor_copy(v2_sg[:], tab2s_win[:].bitcast(U8).indirect(offs2_t[:]))
         for quad in QUADRANTS:
             move_tab2_scale_rows(quad)
         for a in range(KA):
-            load_w1(a, 1)
+            load_w1_half(a, 1)
         for b in range(HB):
             load_words(tab2_win[b], tab2_words[b])
 
-        phase0 = [bank(t, "phase0%d" % t) for t in range(4)]
-        amp0 = [bank(4 + t, "amp0%d" % t) for t in range(4)]
-        gather_tab_words(0)
-        deal_w4_words(0)
-        cast_w1(nc.scalar.copy, 0, 0, 0, P)
-        quantize_w1(0, 0)
-        deal_w4_scales(0)
-        phase_passes(phase0, 0, 0)
-        amp_passes(amp0, 0, 0)
-        gather_tab_words(1)
-        amp_passes(amp0, 1, 0)
-        gather_tab_words(2)
-        amp_passes(amp0, 2, 0)
-        cast_w1(nc.vector.tensor_copy, 1, 0, 0, P)
-        quantize_w1(1, 0)
-        phase_passes(phase0, 1, 0)
-        deal_w4_words(1)
-        deal_w4_scales(1)
-        amp0_sb = sb("amp0_sb", [P, 4, S], F32, tag="w1_raw00")
-        for t in range(4):
-            nc.scalar.copy(amp0_sb[:, t, :], amp0[t][:])
-        turned = bank(5, "turned")
-        nc.tensor.transpose(turned[:, 0:P], rows[:], ident[:])
-        cast_w1(nc.vector.tensor_copy, 2, 0, 0, P)
-        quantize_w1(2, 0)
-        phase_passes(phase0, 2, 0)
-        sines(phase0, 0, 0)
-        cols = sb("cols", [P, 2 * NT], F32, tag="w1_w20")
-        nc.scalar.copy(cols[:], turned[:, VEC_ROW0:P])
-        amp1_wide = [bank(4 + u, "amp1_wide%d" % u) for u in range(2)]
-        for u in range(2):
-            for t in (2 * u, 2 * u + 1):
-                for a in range(KA):
-                    amp_pass(amp1_wide[u][:, (t % 2) * HALF : (t % 2 + 1) * HALF], a, 1, t, slice(0, HALF))
-        sines(phase0, 0, HALF)
+        amp_banks = {b: [bank(4 * b + g, "ampt%d%d" % (b, g)) for g in range(NJ)] for b in (1, 0)}
+        for a in range(KA):
+            for b in (1, 0):
+                amp_passes(amp_banks[b], a, b)
+        for b in (1, 0):
+            park(amp_banks[b], b, ())
 
-        phase1 = [bank(n, "phase1%d" % n) for n in (6, 7, 2, 3)]
-        cast_w1(nc.vector.tensor_copy, 0, 1, 0, P)
+        phase0 = [bank(4 + t, "phase0%d" % t) for t in range(4)]
+        for a in range(KA):
+            if a == KA - 1:
+                amp0 = [turn_amp(0, g) for g in range(NJ)]
+            if a < KA - 1:
+                cast_w1(nc.vector.tensor_copy, a, 0)
+                quantize_w1(a, 0)
+                phase_passes(phase0, a, 0)
+        for t0 in (0, 2):
+            cast_w1(nc.vector.tensor_copy, 2, 0, t0=t0, t1=t0 + 2)
+            quantize_w1(2, 0, t0, t0 + 2)
+            phase_passes(phase0, 2, 0, t0, t0 + 2)
+        sines(phase0, 0)
+
+        phase1 = [bank(4 + t, "phase1%d" % t) for t in range(4)]
+        cast_w1(nc.vector.tensor_copy, 0, 1)
         quantize_w1(0, 1)
         phase_passes(phase1, 0, 1)
-        amp1 = {2 + jc: bank(jc, "amp1%d" % (2 + jc)) for jc in range(2)}
-        cast_w1_shared(1, 1)
+        product(amp0[0], 0, 0, tag="w1_bf01")
+        cast_shared(1, 1, 64)
+        product(amp0[1], 0, 1)
         quantize_w1(1, 1)
         phase_passes(phase1, 1, 1)
-        h0a = sb("h0a", [P, 4 * HALF], BF16, tag="w1_bf01")
-        product(h0a[:], amp0_sb[:, :, 0:HALF], 0, 0, HALF)
-        cast_w1_shared(2, 1)
-        amp1_sb = sb("amp1_sb", [P, 4, HALF], F32, tag="w1_raw21")
-        for u in range(2):
-            nc.scalar.copy(amp1_sb[:, 2 * u : 2 * u + 2, :].rearrange("p t j -> p (t j)"), amp1_wide[u][:])
-        quantize_w1(2, 1)
-        phase_passes(phase1, 2, 1)
-        for jc in range(2, 4):
-            amp_bank(amp1[jc], 1, jc)
-        h0b = sb("h0b", [P, 4 * HALF], BF16, tag="w1_bf21")
-        quantize_h(h0a[:], 0, 0)
-        product(h0b[:], amp0_sb[:, :, HALF:S], 0, HALF, S)
-        quantize_h(h0b[:], 0, HALF)
-        sines(phase1, 1, 0)
-        sines(phase1, 1, HALF)
-        gather_tab2_words(0, 0)
-        h1 = sb("h1", [P, 4 * S], BF16)
-        product(h1[:, 0 : 4 * HALF], amp1_sb[:], 1, 0, HALF)
-        for jc in range(2, 4):
-            amp = amp1[jc][:].rearrange("p (t j) -> p t j", t=4)
-            product(h1[:, jc * PASS : (jc + 1) * PASS], amp, 1, jc * P, (jc + 1) * P)
-            j0 = (jc - 2) * HALF
-            quantize_h(h1[:, 4 * j0 : 4 * (j0 + HALF)], 1, j0)
+        product(amp0[2], 0, 2, tag="w1_bf11")
+        cast_w1(nc.vector.tensor_copy, 2, 1, t0=0, t1=2)
+        cast_w1(nc.scalar.copy, 2, 1, t0=2, t1=4)
+        for t0 in (0, 2):
+            quantize_w1(2, 1, t0, t0 + 2)
+            phase_passes(phase1, 2, 1, t0, t0 + 2)
+        sines(phase1, 1)
+        turned = bank(7, "turned")
+        nc.tensor.transpose(turned[:, 0:P], rows[:], ident[:])
+        nc.scalar.copy(cols[:], turned[:, VEC_ROW0:P])
+        product(amp0[3], 0, 3)
+        quantize_h(0, 0, tag="w1_bf21")
+        quantize_h(0, 1)
+        amp1 = [turn_amp(1, g) for g in range(NJ)]
+        product(amp1[0], 1, 0)
+        product(amp1[1], 1, 1)
+        gather_tab2_words(0, 0, 2, tag="sine10")
+        product(amp1[2], 1, 2)
+        quantize_h(1, 0)
+        gather_tab2_words(0, 2, 4, tag="h_bf10")
+        product(amp1[3], 1, 3)
+        quantize_h(1, 1)
 
         every = slice(0, S)
         halves = (slice(0, HALF), slice(HALF, S))
-        lead = [bank(n, "lead%d" % n) for n in (4, 3)]
-        acc = {c: bank(n, "acc%d" % c) for c, n in ((1, 5), (2, 0), (3, 1), (4, 6), (5, 7), (6, 2))}
+        res = [sb("res%d" % c, [P, S], F32) for c in range(NT)]
+        lead = [bank(4 + n, "lead%d" % n) for n in range(2)]
+        acc = {c: bank(n, "acc%d" % c) for c, n in ((1, 6), (2, 7), (3, 0), (4, 1), (5, 2), (6, 3))}
         for n in range(2):
             out_pass(lead[n][:, 0:HALF], 0, 0, halves[n], True)
         for c in range(1, 4):
             out_pass(acc[c][:], 0, c, every, True)
-        gather_tab2_words(0, 1)
-        for c in range(4, NT - 1):
-            out_pass(acc[c][:], 0, c, every, True)
-        gather_tab2_words(1, 0, tag="tab2_win0")
+        gather_tab2_words(1, 0, 2)
         for n in range(2):
             out_pass(lead[n][:, 0:HALF], 1, 0, halves[n], False)
-        for c in range(1, 4):
-            out_pass(acc[c][:], 1, c, every, False)
-        for n in range(2):
             finish(res[0][:, halves[n]], lead[n][:, 0:HALF], 0, False)
             nc.sync.dma_start(out[0:P, halves[n]], res[0][:, halves[n]])
-        for c in range(1, 4):
-            finish(res[c][:], acc[c][:], c, False)
-            nc.sync.dma_start(out[c * P : (c + 1) * P, :], res[c][:])
         acc[NT - 1] = bank(4, "acc7")
-        out_pass(acc[NT - 1][:], 0, NT - 1, every, True)
-        gather_tab2_words(1, 1)
-        for c in range(4, NT):
-            out_pass(acc[c][:], 1, c, every, False)
-        for c in range(4, NT):
-            finish(res[c][:], acc[c][:], c, c < NT - 1)
+
+        def close(b, c, on_vector):
+            out_pass(acc[c][:], b, c, every, False)
+            finish(res[c][:], acc[c][:], c, on_vector)
             nc.sync.dma_start(out[c * P : (c + 1) * P, :], res[c][:])
+
+        close(1, 1, False)
+        gather_tab2_words(1, 2, 4)
+        close(1, 2, False)
+        close(1, 3, False)
+        for c0 in (4, 6):
+            gather_tab2_words(1, c0, c0 + 2)
+            for c in (c0, c0 + 1):
+                out_pass(acc[c][:], 1, c, every, True)
+            gather_tab2_words(0, c0, c0 + 2, tag="v2_w1%d" % (c0 - 4))
+            for c in (c0, c0 + 1):
+                close(0, c, c == NT - 1)

@@ -71,7 +71,9 @@ def tile_list_mesh_deeponet_sine_kernel(
         w1_w = {(a, b): sb("w1_w%d%d" % (a, b), [P, PASS], U32) for a in range(KA) for b in range(HB)}
         w1_s = [[sb("w1_s%d%d" % (a, b), [P, PASS], U8) for b in range(HB)] for a in range(KA)]
         amp_t = [[sb("amp_t%d%d" % (b, g), [P, PASS], F32) for g in range(NJ)] for b in range(HB)]
-        sine = [[sb("sine%d%d" % (b, u), [P, 4, HALF], F32) for u in range(2)] for b in range(HB)]
+        sine0 = sb("sine0", [P, 4, S], F32)
+        sine1 = [sb("sine1%d" % u, [P, 4, HALF], F32) for u in range(2)]
+        sine = [[sine0[:, :, u * HALF : (u + 1) * HALF] for u in range(2)], [sine1[u][:] for u in range(2)]]
         h_bf = {}
         h_w = {}
         h_s = [sb("h_s%d" % b, [P, S], U8) for b in range(HB)]
@@ -150,7 +152,7 @@ def tile_list_mesh_deeponet_sine_kernel(
                 )
 
         def turn_amp(b, g):
-            dst = bank(g, "amp%d%d" % (b, g))
+            dst = bank(4 + g, "amp%d%d" % (b, g))
             for t in range(4):
                 m = slice(t * P, (t + 1) * P)
                 nc.tensor.transpose(dst[:, m], amp_t[b][g][:, m], ident[:])
@@ -169,11 +171,12 @@ def tile_list_mesh_deeponet_sine_kernel(
                     stop=(a == KA - 1),
                 )
 
-        def sines(banks, b):
-            for u in range(2):
-                j = slice(u * HALF, (u + 1) * HALF)
+        def sines(banks, b, parts):
+            for u in range(parts):
+                j = slice(u * S // parts, (u + 1) * S // parts)
                 for t in range(4):
-                    nc.scalar.activation(sine[b][u][:, t, :], banks[t][:, j], ACT.Sin, bias=bias[:, b, t : t + 1])
+                    dst = sine0[:, t, :] if parts == 1 else sine1[u][:, t, :]
+                    nc.scalar.activation(dst, banks[t][:, j], ACT.Sin, bias=bias[:, b, t : t + 1])
 
         def product(amp, b, g, tag=None):
             u, n = divmod(g, 2)
@@ -216,6 +219,8 @@ def tile_list_mesh_deeponet_sine_kernel(
         nc.gpsimd.memset(w4_s[:].bitcast(I32), 0)
         nc.gpsimd.memset(rows[0:VEC_ROW0], 0.0)
         make_identity(nc, ident[:])
+        warm = sb("warm", [P, 1], F32)
+        nc.scalar.activation(warm[:], ident[:, 0:1], ACT.Sin)
 
         nc.sync.dma_start(offs_t[:], offs)
         nc.sync.dma_start(tabs_win[TAB_ROW0 + BLOCKS : P], tab_scales[0:2].rearrange("a q t -> q a t").bitcast(I32))
@@ -259,20 +264,18 @@ def tile_list_mesh_deeponet_sine_kernel(
             park(amp_banks[b], b, ())
 
         phase0 = [bank(4 + t, "phase0%d" % t) for t in range(4)]
-        for a in range(KA):
-            if a == KA - 1:
-                amp0 = [turn_amp(0, g) for g in range(NJ)]
-            if a < KA - 1:
-                cast_w1(nc.vector.tensor_copy, a, 0)
-                quantize_w1(a, 0)
-                phase_passes(phase0, a, 0)
+        for a in range(KA - 1):
+            cast_w1(nc.vector.tensor_copy, a, 0)
+            quantize_w1(a, 0)
+            phase_passes(phase0, a, 0)
         for t0 in (0, 2):
             cast_w1(nc.vector.tensor_copy, 2, 0, t0=t0, t1=t0 + 2)
             quantize_w1(2, 0, t0, t0 + 2)
             phase_passes(phase0, 2, 0, t0, t0 + 2)
-        sines(phase0, 0)
+        sines(phase0, 0, 1)
+        amp0 = [turn_amp(0, g) for g in range(NJ)]
 
-        phase1 = [bank(4 + t, "phase1%d" % t) for t in range(4)]
+        phase1 = [bank(t, "phase1%d" % t) for t in range(4)]
         cast_w1(nc.vector.tensor_copy, 0, 1)
         quantize_w1(0, 1)
         phase_passes(phase1, 0, 1)
@@ -281,18 +284,18 @@ def tile_list_mesh_deeponet_sine_kernel(
         product(amp0[1], 0, 1)
         quantize_w1(1, 1)
         phase_passes(phase1, 1, 1)
-        product(amp0[2], 0, 2, tag="w1_bf11")
         cast_w1(nc.vector.tensor_copy, 2, 1, t0=0, t1=2)
         cast_w1(nc.scalar.copy, 2, 1, t0=2, t1=4)
         for t0 in (0, 2):
             quantize_w1(2, 1, t0, t0 + 2)
             phase_passes(phase1, 2, 1, t0, t0 + 2)
-        sines(phase1, 1)
-        turned = bank(7, "turned")
+        sines(phase1, 1, 2)
+        turned = bank(3, "turned")
         nc.tensor.transpose(turned[:, 0:P], rows[:], ident[:])
         nc.scalar.copy(cols[:], turned[:, VEC_ROW0:P])
+        product(amp0[2], 0, 2, tag="w1_bf21")
+        quantize_h(0, 0, tag="w1_half21")
         product(amp0[3], 0, 3)
-        quantize_h(0, 0, tag="w1_bf21")
         quantize_h(0, 1)
         amp1 = [turn_amp(1, g) for g in range(NJ)]
         product(amp1[0], 1, 0)
@@ -307,8 +310,8 @@ def tile_list_mesh_deeponet_sine_kernel(
         every = slice(0, S)
         halves = (slice(0, HALF), slice(HALF, S))
         res = [sb("res%d" % c, [P, S], F32) for c in range(NT)]
-        lead = [bank(4 + n, "lead%d" % n) for n in range(2)]
-        acc = {c: bank(n, "acc%d" % c) for c, n in ((1, 6), (2, 7), (3, 0), (4, 1), (5, 2), (6, 3))}
+        lead = [bank(n, "lead%d" % n) for n in range(2)]
+        acc = {c: bank(n, "acc%d" % c) for c, n in ((1, 2), (2, 3), (3, 4), (4, 5), (5, 6), (6, 7))}
         for n in range(2):
             out_pass(lead[n][:, 0:HALF], 0, 0, halves[n], True)
         for c in range(1, 4):
@@ -318,7 +321,7 @@ def tile_list_mesh_deeponet_sine_kernel(
             out_pass(lead[n][:, 0:HALF], 1, 0, halves[n], False)
             finish(res[0][:, halves[n]], lead[n][:, 0:HALF], 0, False)
             nc.sync.dma_start(out[0:P, halves[n]], res[0][:, halves[n]])
-        acc[NT - 1] = bank(4, "acc7")
+        acc[NT - 1] = bank(0, "acc7")
 
         def close(b, c, on_vector):
             out_pass(acc[c][:], b, c, every, False)

@@ -219,8 +219,6 @@ def tile_list_mesh_deeponet_sine_kernel(
         nc.gpsimd.memset(w4_s[:].bitcast(I32), 0)
         nc.gpsimd.memset(rows[0:VEC_ROW0], 0.0)
         make_identity(nc, ident[:])
-        warm = sb("warm", [P, 1], F32)
-        nc.scalar.activation(warm[:], ident[:, 0:1], ACT.Sin)
 
         nc.sync.dma_start(offs_t[:], offs)
         nc.sync.dma_start(tabs_win[TAB_ROW0 + BLOCKS : P], tab_scales[0:2].rearrange("a q t -> q a t").bitcast(I32))

@@ -26,7 +26,8 @@ NJ = S // P
 BLOCKS = PASS // 32
 HALF = S // 2
 PAIR = 2 * P
-TAB_ROW0 = P - KA * BLOCKS
+TAB_ROW0 = 32
+TAB_LAST_ROW0 = 16
 TAB2_ROW0 = P - HB * BLOCKS
 VEC_ROW0 = P - 2 * NT
 V2_PLANE = 4
@@ -90,11 +91,11 @@ def tile_list_mesh_deeponet_sine_kernel(
             nc.sync.dma_start(w4_s[r:P:32].bitcast(I32), src.bitcast(I32))
 
         def move_tab_scale_rows(quad):
-            first = TAB_ROW0 + BLOCKS + 8 * quad
+            first = TAB_ROW0 + 8 * quad
             nc.sync.dma_start(v_s[32 * quad : 32 * quad + 4, 0:2], v_sg[first : first + 8].bitcast(I32))
 
         def move_last_tab_scale_rows(quad):
-            first = TAB_ROW0 + 4 * quad
+            first = TAB_LAST_ROW0 + 4 * quad
             nc.sync.dma_start(v_s[32 * quad : 32 * quad + 4, 2], v_sg[first : first + 4].bitcast(I32))
 
         def move_tab2_scale_rows(quad):
@@ -104,6 +105,11 @@ def tile_list_mesh_deeponet_sine_kernel(
 
         def gather_tab_words(a):
             nc.vector.tensor_copy(v_w[a][:], tab_win[a][:].bitcast(U32).indirect(offs_t[:]))
+
+        def gather_tab2_scale_rows(n):
+            nc.vector.tensor_copy(
+                v2_sg[:, n * PASS : (n + 1) * PASS], tab2s_win[:].bitcast(U8).indirect(offs2_t[:, n * 32 : (n + 1) * 32])
+            )
 
         def gather_tab2_words(b, c0, c1, tag=None):
             tile = sb("v2_w%d%d" % (b, c0), [P, (c1 - c0) * P], U32, tag=tag)
@@ -213,7 +219,8 @@ def tile_list_mesh_deeponet_sine_kernel(
             else:
                 nc.scalar.activation(dst, acc, ACT.Identity, bias=shift, scale=scale)
 
-        nc.vector.memset(tabs_win[0:TAB_ROW0], 0)
+        nc.vector.memset(tabs_win[0:TAB_LAST_ROW0], 0)
+        nc.vector.memset(tabs_win[TAB_ROW0 + 2 * BLOCKS : P], 0)
         nc.vector.memset(v_s[:], 0)
         nc.vector.memset(tab2s_win[0:TAB2_ROW0], 0)
         nc.gpsimd.memset(w4_s[:].bitcast(I32), 0)
@@ -221,32 +228,32 @@ def tile_list_mesh_deeponet_sine_kernel(
         make_identity(nc, ident[:])
 
         nc.sync.dma_start(offs_t[:], offs)
-        nc.sync.dma_start(tabs_win[TAB_ROW0 + BLOCKS : P], tab_scales[0:2].rearrange("a q t -> q a t").bitcast(I32))
-        nc.sync.dma_start(tabs_win[TAB_ROW0 : TAB_ROW0 + BLOCKS], tab_scales[2].bitcast(I32))
+        nc.sync.dma_start(tabs_win[TAB_ROW0 : TAB_ROW0 + 2 * BLOCKS], tab_scales[0:2].rearrange("a q t -> q a t").bitcast(I32))
+        nc.sync.dma_start(tabs_win[TAB_LAST_ROW0:TAB_ROW0], tab_scales[2].bitcast(I32))
         nc.sync.dma_start(w4_w[:].bitcast(I32), w4_words.rearrange("a p n -> p a n").bitcast(I32))
         for r in range(4):
             load_w4_scale_rows(r)
         load_words(tab_win[0], tab_words[0])
         nc.sync.dma_start(offs2_t[:], offs2)
         nc.sync.dma_start(tab2s_win[TAB2_ROW0:P], tab2_scales.rearrange("b q t -> q b t").bitcast(I32))
-        load_words(tab_win[1], tab_words[1])
         nc.vector.tensor_copy(v_sg[:], tabs_win[:].bitcast(U8).indirect(offs_t[:]))
         v2_s = sb("v2_s", [P, HB, S2 // 4], I32, tag="tabs_win")
         for quad in QUADRANTS:
             move_tab_scale_rows(quad)
         nc.gpsimd.memset(v2_s[:], 0)
+        load_words(tab_win[1], tab_words[1])
         load_words(tab_win[2], tab_words[2])
-        load_w1_half(0, 0)
         for quad in QUADRANTS:
             move_last_tab_scale_rows(quad)
-        load_w1_half(1, 0)
-        load_w1_half(2, 0)
+        for a in range(KA):
+            load_w1_half(a, 0)
         nc.sync.dma_start(rows[VEC_ROW0 : VEC_ROW0 + NT, :], mask.rearrange("(c p) -> c p", p=P))
         nc.sync.dma_start(rows[VEC_ROW0 + NT : P, :], bval.rearrange("(c p) -> c p", p=P))
         nc.sync.dma_start(bias[:], b1.rearrange("(b p t) -> p b t", b=HB, t=4))
         for a in range(KA):
             gather_tab_words(a)
-        nc.vector.tensor_copy(v2_sg[:], tab2s_win[:].bitcast(U8).indirect(offs2_t[:]))
+            if a < 2:
+                gather_tab2_scale_rows(a)
         for quad in QUADRANTS:
             move_tab2_scale_rows(quad)
         for a in range(KA):
@@ -294,15 +301,15 @@ def tile_list_mesh_deeponet_sine_kernel(
         product(amp0[2], 0, 2, tag="w1_bf21")
         quantize_h(0, 0, tag="w1_half21")
         product(amp0[3], 0, 3)
-        quantize_h(0, 1)
         amp1 = [turn_amp(1, g) for g in range(NJ)]
         product(amp1[0], 1, 0)
+        quantize_h(0, 1)
         product(amp1[1], 1, 1)
         gather_tab2_words(0, 0, 2, tag="sine10")
         product(amp1[2], 1, 2)
         quantize_h(1, 0)
-        gather_tab2_words(0, 2, 4, tag="h_bf10")
         product(amp1[3], 1, 3)
+        gather_tab2_words(0, 2, 4, tag="h_bf10")
         quantize_h(1, 1)
 
         every = slice(0, S)

@@ -177,6 +177,27 @@ def tile_list_mesh_deeponet_sine_kernel(
                     stop=(a == KA - 1),
                 )
 
+        def half_phase_passes(banks, a, t0):
+            for u in range(2):
+                j = slice(u * HALF, (u + 1) * HALF)
+                for t in (t0, t0 + 1):
+                    m = slice(t * P, (t + 1) * P)
+                    nc.tensor.matmul_mx(
+                        banks[t0, u][:, (t - t0) * HALF : (t - t0 + 1) * HALF],
+                        lhsT=w1_w[a, 1][:, m].bitcast(FP8X4),
+                        lhsT_scale=w1_s[a][1][:, m],
+                        rhs=v_w[a][:, j].bitcast(FP8X4),
+                        rhs_scale=v_s[:, a, :].bitcast(U8)[:, j],
+                        start=(a == 0 and t == t0),
+                        stop=(a == KA - 1 and t == t0 + 1),
+                    )
+
+        def half_sines(banks):
+            for u in range(2):
+                for t in range(4):
+                    src = banks[t - t % 2, u][:, (t % 2) * HALF : (t % 2 + 1) * HALF]
+                    nc.scalar.activation(sine1[u][:, t, :], src, ACT.Sin, bias=bias[:, 1, t : t + 1])
+
         def sines(banks, b, parts):
             for u in range(parts):
                 j = slice(u * S // parts, (u + 1) * S // parts)
@@ -236,16 +257,17 @@ def tile_list_mesh_deeponet_sine_kernel(
         load_words(tab_win[0], tab_words[0])
         nc.sync.dma_start(offs2_t[:], offs2)
         nc.sync.dma_start(tab2s_win[TAB2_ROW0:P], tab2_scales.rearrange("b q t -> q b t").bitcast(I32))
+        load_words(tab_win[1], tab_words[1])
         nc.vector.tensor_copy(v_sg[:], tabs_win[:].bitcast(U8).indirect(offs_t[:]))
         v2_s = sb("v2_s", [P, HB, S2 // 4], I32, tag="tabs_win")
         for quad in QUADRANTS:
             move_tab_scale_rows(quad)
         nc.gpsimd.memset(v2_s[:], 0)
-        load_words(tab_win[1], tab_words[1])
         load_words(tab_win[2], tab_words[2])
+        load_w1_half(0, 0)
         for quad in QUADRANTS:
             move_last_tab_scale_rows(quad)
-        for a in range(KA):
+        for a in range(1, KA):
             load_w1_half(a, 0)
         nc.sync.dma_start(rows[VEC_ROW0 : VEC_ROW0 + NT, :], mask.rearrange("(c p) -> c p", p=P))
         nc.sync.dma_start(rows[VEC_ROW0 + NT : P, :], bval.rearrange("(c p) -> c p", p=P))
@@ -280,21 +302,24 @@ def tile_list_mesh_deeponet_sine_kernel(
         sines(phase0, 0, 1)
         amp0 = [turn_amp(0, g) for g in range(NJ)]
 
-        phase1 = [bank(t, "phase1%d" % t) for t in range(4)]
+        phase1 = {(t0, u): bank(t0 // 2 + 2 * u, "phase1%d%d" % (t0, u)) for t0 in (0, 2) for u in range(2)}
         cast_w1(nc.vector.tensor_copy, 0, 1)
         quantize_w1(0, 1)
-        phase_passes(phase1, 0, 1)
+        for t0 in (0, 2):
+            half_phase_passes(phase1, 0, t0)
         product(amp0[0], 0, 0, tag="w1_bf01")
         cast_shared(1, 1, 64)
         product(amp0[1], 0, 1)
         quantize_w1(1, 1)
-        phase_passes(phase1, 1, 1)
+        for t0 in (0, 2):
+            half_phase_passes(phase1, 1, t0)
         cast_w1(nc.vector.tensor_copy, 2, 1, t0=0, t1=2)
-        cast_w1(nc.scalar.copy, 2, 1, t0=2, t1=4)
+        cast_w1(nc.vector.tensor_copy, 2, 1, 0, 40, t0=2, t1=4)
+        cast_w1(nc.scalar.copy, 2, 1, 40, P, t0=2, t1=4)
         for t0 in (0, 2):
             quantize_w1(2, 1, t0, t0 + 2)
-            phase_passes(phase1, 2, 1, t0, t0 + 2)
-        sines(phase1, 1, 2)
+            half_phase_passes(phase1, 2, t0)
+        half_sines(phase1)
         turned = bank(3, "turned")
         nc.tensor.transpose(turned[:, 0:P], rows[:], ident[:])
         nc.scalar.copy(cols[:], turned[:, VEC_ROW0:P])

@@ -249,8 +249,8 @@ def tile_list_mesh_deeponet_sine_kernel(
         make_identity(nc, ident[:])
 
         nc.sync.dma_start(offs_t[:], offs)
-        nc.sync.dma_start(tabs_win[TAB_ROW0 : TAB_ROW0 + 2 * BLOCKS], tab_scales[0:2].rearrange("a q t -> q a t").bitcast(I32))
-        nc.sync.dma_start(tabs_win[TAB_LAST_ROW0:TAB_ROW0], tab_scales[2].bitcast(I32))
+        nc.scalar.dma_start(tabs_win[TAB_ROW0 : TAB_ROW0 + 2 * BLOCKS], tab_scales[0:2].rearrange("a q t -> q a t").bitcast(I32))
+        nc.scalar.dma_start(tabs_win[TAB_LAST_ROW0:TAB_ROW0], tab_scales[2].bitcast(I32))
         nc.sync.dma_start(w4_w[:].bitcast(I32), w4_words.rearrange("a p n -> p a n").bitcast(I32))
         for r in range(4):
             load_w4_scale_rows(r)
@@ -308,7 +308,7 @@ def tile_list_mesh_deeponet_sine_kernel(
         for t0 in (0, 2):
             half_phase_passes(phase1, 0, t0)
         product(amp0[0], 0, 0, tag="w1_bf01")
-        cast_shared(1, 1, 64)
+        cast_shared(1, 1, 32)
         product(amp0[1], 0, 1)
         quantize_w1(1, 1)
         for t0 in (0, 2):
@@ -339,9 +339,10 @@ def tile_list_mesh_deeponet_sine_kernel(
 
         every = slice(0, S)
         halves = (slice(0, HALF), slice(HALF, S))
-        res = [sb("res%d" % c, [P, S], F32) for c in range(NT)]
+        res = {c: sb("res%d" % c, [P, 1, S], F32) for c in range(NT - 2)}
+        res[NT - 2] = sb("res_last", [P, 2, S], F32)
         lead = [bank(n, "lead%d" % n) for n in range(2)]
-        acc = {c: bank(n, "acc%d" % c) for c, n in ((1, 2), (2, 3), (3, 4), (4, 5), (5, 6), (6, 7))}
+        acc = {c: bank(c + 1, "acc%d" % c) for c in range(1, NT - 1)}
         for n in range(2):
             out_pass(lead[n][:, 0:HALF], 0, 0, halves[n], True)
         for c in range(1, 4):
@@ -349,23 +350,26 @@ def tile_list_mesh_deeponet_sine_kernel(
         gather_tab2_words(1, 0, 2)
         for n in range(2):
             out_pass(lead[n][:, 0:HALF], 1, 0, halves[n], False)
-            finish(res[0][:, halves[n]], lead[n][:, 0:HALF], 0, False)
-            nc.sync.dma_start(out[0:P, halves[n]], res[0][:, halves[n]])
+            finish(res[0][:, 0, halves[n]], lead[n][:, 0:HALF], 0, False)
+            nc.sync.dma_start(out[0:P, halves[n]], res[0][:, 0, halves[n]])
         acc[NT - 1] = bank(0, "acc7")
 
-        def close(b, c, on_vector):
+        def close(b, c):
+            first = min(c, NT - 2)
             out_pass(acc[c][:], b, c, every, False)
-            finish(res[c][:], acc[c][:], c, on_vector)
-            nc.sync.dma_start(out[c * P : (c + 1) * P, :], res[c][:])
+            finish(res[first][:, c - first, :], acc[c][:], c, c in (5, 7))
+            if c != NT - 2:
+                dst = out[first * P : (c + 1) * P, :].rearrange("(c p) n -> p c n", p=P)
+                nc.sync.dma_start(dst, res[first][:])
 
-        close(1, 1, False)
+        close(1, 1)
         gather_tab2_words(1, 2, 4)
-        close(1, 2, False)
-        close(1, 3, False)
+        close(1, 2)
+        close(1, 3)
         for c0 in (4, 6):
             gather_tab2_words(1, c0, c0 + 2)
             for c in (c0, c0 + 1):
                 out_pass(acc[c][:], 1, c, every, True)
             gather_tab2_words(0, c0, c0 + 2, tag="v2_w1%d" % (c0 - 4))
-            for c in (c0, c0 + 1):
-                close(0, c, c == NT - 1)
+        for c in range(4, NT):
+            close(0, c)

from contextlib import ExitStack

import concourse.mybir as mybir
from concourse.masks import make_identity

K, T, S, H, T2, S2 = 1536, 2048, 512, 1024, 4096, 1024
FLOPS = 2 * (2 * K * H * S + H * S2 * S)

F32 = mybir.dt.float32
BF16 = mybir.dt.bfloat16
I32 = mybir.dt.int32
U32 = mybir.dt.uint32
U16 = mybir.dt.uint16
U8 = mybir.dt.uint8
FP8X4 = mybir.dt.float8_e4m3fn_x4
FP4X4 = mybir.dt.float4_e2m1fn_x4
ACT = mybir.ActivationFunctionType
ALU = mybir.AluOpType

P = 128
PASS = 512
KA = K // PASS
HB = H // PASS
NT = S2 // P
NJ = S // P
BLOCKS = PASS // 32
HALF = S // 2
PAIR = 2 * P
TAB_ROW0 = 32
TAB_LAST_ROW0 = 16
TAB2_ROW0 = P - HB * BLOCKS
VEC_ROW0 = P - 2 * NT
V2_PLANE = 4
QUADRANTS = (0, 2, 1, 3)


def tile_list_mesh_deeponet_sine_kernel(
    tc, tab_words, tab_scales, offs, tab2_words, tab2_scales, offs2, w1, b1, w4_words, w4_scales, mask, bval, out
):
    nc = tc.nc
    with ExitStack() as ctx:
        keep = ctx.enter_context(tc.tile_pool(name="keep", bufs=1))
        psum = ctx.enter_context(tc.psum_pool(name="psum", bufs=1))

        def sb(name, shape, dtype, tag=None):
            return keep.tile(shape, dtype, name=name, tag=tag or name, align_bytes=64)

        def bank(n, name):
            return psum.tile([P, PASS], F32, name=name, tag="bank%d" % n)

        offs_t = keep.tile([P, S // 16], U16, name="offs_t")
        offs2_t = keep.tile([P, S2 // 16], U16, name="offs2_t")
        bias = sb("bias", [P, HB, 4], F32)
        rows = sb("rows", [P, P], F32)
        ident = sb("ident", [P, P], F32)
        cols = sb("cols", [P, 2 * NT], F32)

        tab_win = [sb("tab_win%d" % a, [P, T], I32) for a in range(KA)]
        tabs_win = sb("tabs_win", [P, T // 4], I32)
        tab2_win = [sb("tab2_win%d" % b, [P, T2], I32) for b in range(HB)]
        tab2s_win = sb("tab2s_win", [P, T2 // 4], I32)
        w4_w = sb("w4_w", [P, KA, 2 * H], U8)
        w4_s = sb("w4_s", [P, KA, H], U8)
        w1_half = {(a, b): sb("w1_half%d%d" % (a, b), [P, 4, PASS], F32) for a in range(KA) for b in range(HB)}

        v_w = [sb("v_w%d" % a, [P, S], U32) for a in range(KA)]
        v_sg = sb("v_sg", [P, S], U8)
        v_s = sb("v_s", [P, KA, S // 4], I32)
        v2_w = {}
        v2_sg = sb("v2_sg", [P, S2], U8)
        w1_bf = {}
        w1_w = {(a, b): sb("w1_w%d%d" % (a, b), [P, PASS], U32) for a in range(KA) for b in range(HB)}
        w1_s = [[sb("w1_s%d%d" % (a, b), [P, PASS], U8) for b in range(HB)] for a in range(KA)]
        amp_t = [[sb("amp_t%d%d" % (b, g), [P, PASS], F32) for g in range(NJ)] for b in range(HB)]
        sine0 = sb("sine0", [P, 4, S], F32)
        sine1 = [sb("sine1%d" % u, [P, 4, HALF], F32) for u in range(2)]
        sine = [[sine0[:, :, u * HALF : (u + 1) * HALF] for u in range(2)], [sine1[u][:] for u in range(2)]]
        h_bf = {}
        h_w = {}
        h_s = [sb("h_s%d" % b, [P, S], U8) for b in range(HB)]

        def load_words(win, words):
            nc.sync.dma_start(win[:], words.rearrange("p t i -> p (t i)").bitcast(I32))

        def load_w1_half(a, b):
            src = w1[a * PASS : (a + 1) * PASS, b * PASS : (b + 1) * PASS]
            nc.sync.dma_start(w1_half[a, b][:], src.rearrange("(p j) c -> p j c", j=4))

        def load_w4_scale_rows(r):
            src = w4_scales.rearrange("a (q r) t -> r q a t", r=4)[r]
            nc.sync.dma_start(w4_s[r:P:32].bitcast(I32), src.bitcast(I32))

        def move_tab_scale_rows(quad):
            first = TAB_ROW0 + 8 * quad
            nc.sync.dma_start(v_s[32 * quad : 32 * quad + 4, 0:2], v_sg[first : first + 8].bitcast(I32))

        def move_last_tab_scale_rows(quad):
            first = TAB_LAST_ROW0 + 4 * quad
            nc.sync.dma_start(v_s[32 * quad : 32 * quad + 4, 2], v_sg[first : first + 4].bitcast(I32))

        def move_tab2_scale_rows(quad):
            first = TAB2_ROW0 + 4 * HB * quad
            plane = 32 * quad + V2_PLANE
            nc.gpsimd.dma_start(v2_s[plane : plane + 4], v2_sg[first : first + 4 * HB].bitcast(I32))

        def gather_tab_words(a):
            nc.vector.tensor_copy(v_w[a][:], tab_win[a][:].bitcast(U32).indirect(offs_t[:]))

        def gather_tab2_scale_rows(n):
            nc.vector.tensor_copy(
                v2_sg[:, n * PASS : (n + 1) * PASS], tab2s_win[:].bitcast(U8).indirect(offs2_t[:, n * 32 : (n + 1) * 32])
            )

        def gather_tab2_words(b, c0, c1, tag=None):
            tile = sb("v2_w%d%d" % (b, c0), [P, (c1 - c0) * P], U32, tag=tag)
            for c in range(c0, c1):
                v2_w[b, c] = tile[:, (c - c0) * P : (c - c0 + 1) * P]
            nc.vector.tensor_copy(tile[:], tab2_win[b][:].bitcast(U32).indirect(offs2_t[:, c0 * 8 : c1 * 8]))

        def cast_w1(copy, a, b, m0=0, m1=P, t0=0, t1=4):
            if (a, b) not in w1_bf:
                w1_bf[a, b] = sb("w1_bf%d%d" % (a, b), [P, 4 * PASS], BF16)
            raw = w1_half[a, b][:]
            copy(
                w1_bf[a, b][:].rearrange("p (t m j) -> p m j t", t=4, j=4)[:, m0:m1, :, t0:t1],
                raw.rearrange("p j (m t) -> p m j t", t=4)[:, m0:m1, :, t0:t1],
            )

        def cast_shared(a, b, share):
            cast_w1(nc.vector.tensor_copy, a, b, 0, share)
            cast_w1(nc.scalar.copy, a, b, share, P)

        def quantize_w1(a, b, t0=0, t1=4):
            m = slice(t0 * P, t1 * P)
            nc.vector.quantize_mx(
                w1_w[a, b][:, m].bitcast(FP8X4), w1_s[a][b][:, m], w1_bf[a, b][:, 4 * t0 * P : 4 * t1 * P]
            )

        def amp_passes(banks, a, b):
            for g in range(NJ):
                j = slice(g * P, (g + 1) * P)
                nc.tensor.matmul_mx(
                    banks[g][:],
                    lhsT=v_w[a][:, j].bitcast(FP8X4),
                    lhsT_scale=v_s[:, a, :].bitcast(U8)[:, j],
                    rhs=w4_w[:, a, 2 * b * PASS : 2 * (b + 1) * PASS].bitcast(FP4X4),
                    rhs_scale=w4_s[:, a, b * PASS : (b + 1) * PASS],
                    start=(a == 0),
                    stop=(a == KA - 1),
                )

        def park(banks, b, on_vector):
            for g in range(NJ):
                copy = nc.vector.tensor_copy if g in on_vector else nc.scalar.copy
                copy(
                    amp_t[b][g][:].rearrange("p (t m) -> p t m", t=4),
                    banks[g][:].rearrange("p (m t) -> p t m", t=4),
                )

        def turn_amp(b, g):
            dst = bank(4 + g, "amp%d%d" % (b, g))
            for t in range(4):
                m = slice(t * P, (t + 1) * P)
                nc.tensor.transpose(dst[:, m], amp_t[b][g][:, m], ident[:])
            return dst

        def phase_passes(banks, a, b, t0=0, t1=4):
            for t in range(t0, t1):
                m = slice(t * P, (t + 1) * P)
                nc.tensor.matmul_mx(
                    banks[t][:],
                    lhsT=w1_w[a, b][:, m].bitcast(FP8X4),
                    lhsT_scale=w1_s[a][b][:, m],
                    rhs=v_w[a][:].bitcast(FP8X4),
                    rhs_scale=v_s[:, a, :].bitcast(U8),
                    start=(a == 0),
                    stop=(a == KA - 1),
                )

        def half_phase_passes(banks, a, t0):
            for u in range(2):
                j = slice(u * HALF, (u + 1) * HALF)
                for t in (t0, t0 + 1):
                    m = slice(t * P, (t + 1) * P)
                    nc.tensor.matmul_mx(
                        banks[t0, u][:, (t - t0) * HALF : (t - t0 + 1) * HALF],
                        lhsT=w1_w[a, 1][:, m].bitcast(FP8X4),
                        lhsT_scale=w1_s[a][1][:, m],
                        rhs=v_w[a][:, j].bitcast(FP8X4),
                        rhs_scale=v_s[:, a, :].bitcast(U8)[:, j],
                        start=(a == 0 and t == t0),
                        stop=(a == KA - 1 and t == t0 + 1),
                    )

        def half_sines(banks):
            for u in range(2):
                for t in range(4):
                    src = banks[t - t % 2, u][:, (t % 2) * HALF : (t % 2 + 1) * HALF]
                    nc.scalar.activation(sine1[u][:, t, :], src, ACT.Sin, bias=bias[:, 1, t : t + 1])

        def sines(banks, b, parts):
            for u in range(parts):
                j = slice(u * S // parts, (u + 1) * S // parts)
                for t in range(4):
                    dst = sine0[:, t, :] if parts == 1 else sine1[u][:, t, :]
                    nc.scalar.activation(dst, banks[t][:, j], ACT.Sin, bias=bias[:, b, t : t + 1])

        def product(amp, b, g, tag=None):
            u, n = divmod(g, 2)
            if n == 0:
                h_bf[b, u] = sb("h_bf%d%d" % (b, u), [P, 4 * HALF], BF16, tag=tag)
            nc.vector.tensor_tensor(
                h_bf[b, u][:, n * PASS : (n + 1) * PASS].rearrange("p (c i t) -> p c t i", i=4, t=4),
                amp[:].rearrange("p (t c i) -> p c t i", t=4, i=4),
                sine[b][u][:, :, n * P : (n + 1) * P].rearrange("p t (c i) -> p c t i", i=4),
                ALU.mult,
            )

        def quantize_h(b, u, tag=None):
            if u == 0:
                h_w[b] = sb("h_w%d" % b, [P, S], U32, tag=tag)
            j = slice(u * HALF, (u + 1) * HALF)
            nc.vector.quantize_mx(h_w[b][:, j].bitcast(FP8X4), h_s[b][:, j], h_bf[b, u][:])

        def out_pass(dst, b, c, j, first):
            nc.tensor.matmul_mx(
                dst,
                lhsT=v2_w[b, c].bitcast(FP8X4),
                lhsT_scale=v2_s[V2_PLANE:P, b, :].bitcast(U8)[:, c * P : (c + 1) * P],
                rhs=h_w[b][:, j].bitcast(FP8X4),
                rhs_scale=h_s[b][:, j],
                start=first,
                stop=not first,
            )

        def finish(dst, acc, c, on_vector):
            scale, shift = cols[:, c : c + 1], cols[:, NT + c : NT + c + 1]
            if on_vector:
                nc.vector.tensor_scalar(dst, acc, scale, shift, ALU.mult, ALU.add)
            else:
                nc.scalar.activation(dst, acc, ACT.Identity, bias=shift, scale=scale)

        nc.vector.memset(tabs_win[0:TAB_LAST_ROW0], 0)
        nc.vector.memset(tabs_win[TAB_ROW0 + 2 * BLOCKS : P], 0)
        nc.vector.memset(v_s[:], 0)
        nc.vector.memset(tab2s_win[0:TAB2_ROW0], 0)
        nc.gpsimd.memset(w4_s[:].bitcast(I32), 0)
        nc.gpsimd.memset(rows[0:VEC_ROW0], 0.0)
        make_identity(nc, ident[:])

        nc.sync.dma_start(offs_t[:], offs)
        nc.scalar.dma_start(tabs_win[TAB_ROW0 : TAB_ROW0 + 2 * BLOCKS], tab_scales[0:2].rearrange("a q t -> q a t").bitcast(I32))
        nc.scalar.dma_start(tabs_win[TAB_LAST_ROW0:TAB_ROW0], tab_scales[2].bitcast(I32))
        nc.sync.dma_start(w4_w[:].bitcast(I32), w4_words.rearrange("a p n -> p a n").bitcast(I32))
        for r in range(4):
            load_w4_scale_rows(r)
        load_words(tab_win[0], tab_words[0])
        nc.sync.dma_start(offs2_t[:], offs2)
        nc.sync.dma_start(tab2s_win[TAB2_ROW0:P], tab2_scales.rearrange("b q t -> q b t").bitcast(I32))
        load_words(tab_win[1], tab_words[1])
        nc.vector.tensor_copy(v_sg[:], tabs_win[:].bitcast(U8).indirect(offs_t[:]))
        v2_s = sb("v2_s", [P, HB, S2 // 4], I32, tag="tabs_win")
        for quad in QUADRANTS:
            move_tab_scale_rows(quad)
        nc.gpsimd.memset(v2_s[:], 0)
        load_words(tab_win[2], tab_words[2])
        load_w1_half(0, 0)
        for quad in QUADRANTS:
            move_last_tab_scale_rows(quad)
        for a in range(1, KA):
            load_w1_half(a, 0)
        nc.sync.dma_start(rows[VEC_ROW0 : VEC_ROW0 + NT, :], mask.rearrange("(c p) -> c p", p=P))
        nc.sync.dma_start(rows[VEC_ROW0 + NT : P, :], bval.rearrange("(c p) -> c p", p=P))
        nc.sync.dma_start(bias[:], b1.rearrange("(b p t) -> p b t", b=HB, t=4))
        for a in range(KA):
            gather_tab_words(a)
            if a < 2:
                gather_tab2_scale_rows(a)
        for quad in QUADRANTS:
            move_tab2_scale_rows(quad)
        for a in range(KA):
            load_w1_half(a, 1)
        for b in range(HB):
            load_words(tab2_win[b], tab2_words[b])

        amp_banks = {b: [bank(4 * b + g, "ampt%d%d" % (b, g)) for g in range(NJ)] for b in (1, 0)}
        for a in range(KA):
            for b in (1, 0):
                amp_passes(amp_banks[b], a, b)
        for b in (1, 0):
            park(amp_banks[b], b, ())

        phase0 = [bank(4 + t, "phase0%d" % t) for t in range(4)]
        for a in range(KA - 1):
            cast_w1(nc.vector.tensor_copy, a, 0)
            quantize_w1(a, 0)
            phase_passes(phase0, a, 0)
        for t0 in (0, 2):
            cast_w1(nc.vector.tensor_copy, 2, 0, t0=t0, t1=t0 + 2)
            quantize_w1(2, 0, t0, t0 + 2)
            phase_passes(phase0, 2, 0, t0, t0 + 2)
        sines(phase0, 0, 1)
        amp0 = [turn_amp(0, g) for g in range(NJ)]

        phase1 = {(t0, u): bank(t0 // 2 + 2 * u, "phase1%d%d" % (t0, u)) for t0 in (0, 2) for u in range(2)}
        cast_w1(nc.vector.tensor_copy, 0, 1)
        quantize_w1(0, 1)
        for t0 in (0, 2):
            half_phase_passes(phase1, 0, t0)
        product(amp0[0], 0, 0, tag="w1_bf01")
        cast_shared(1, 1, 32)
        product(amp0[1], 0, 1)
        quantize_w1(1, 1)
        for t0 in (0, 2):
            half_phase_passes(phase1, 1, t0)
        cast_w1(nc.vector.tensor_copy, 2, 1, t0=0, t1=2)
        cast_w1(nc.vector.tensor_copy, 2, 1, 0, 40, t0=2, t1=4)
        cast_w1(nc.scalar.copy, 2, 1, 40, P, t0=2, t1=4)
        for t0 in (0, 2):
            quantize_w1(2, 1, t0, t0 + 2)
            half_phase_passes(phase1, 2, t0)
        half_sines(phase1)
        turned = bank(3, "turned")
        nc.tensor.transpose(turned[:, 0:P], rows[:], ident[:])
        nc.scalar.copy(cols[:], turned[:, VEC_ROW0:P])
        product(amp0[2], 0, 2, tag="w1_bf21")
        quantize_h(0, 0, tag="w1_half21")
        product(amp0[3], 0, 3)
        amp1 = [turn_amp(1, g) for g in range(NJ)]
        product(amp1[0], 1, 0)
        quantize_h(0, 1)
        product(amp1[1], 1, 1)
        gather_tab2_words(0, 0, 2, tag="sine10")
        product(amp1[2], 1, 2)
        quantize_h(1, 0)
        product(amp1[3], 1, 3)
        gather_tab2_words(0, 2, 4, tag="h_bf10")
        quantize_h(1, 1)

        every = slice(0, S)
        halves = (slice(0, HALF), slice(HALF, S))
        res = {c: sb("res%d" % c, [P, 1, S], F32) for c in range(NT - 2)}
        res[NT - 2] = sb("res_last", [P, 2, S], F32)
        lead = [bank(n, "lead%d" % n) for n in range(2)]
        acc = {c: bank(c + 1, "acc%d" % c) for c in range(1, NT - 1)}
        for n in range(2):
            out_pass(lead[n][:, 0:HALF], 0, 0, halves[n], True)
        for c in range(1, 4):
            out_pass(acc[c][:], 0, c, every, True)
        gather_tab2_words(1, 0, 2)
        for n in range(2):
            out_pass(lead[n][:, 0:HALF], 1, 0, halves[n], False)
            finish(res[0][:, 0, halves[n]], lead[n][:, 0:HALF], 0, False)
            nc.sync.dma_start(out[0:P, halves[n]], res[0][:, 0, halves[n]])
        acc[NT - 1] = bank(0, "acc7")

        def close(b, c):
            first = min(c, NT - 2)
            out_pass(acc[c][:], b, c, every, False)
            finish(res[first][:, c - first, :], acc[c][:], c, c in (5, 7))
            if c != NT - 2:
                dst = out[first * P : (c + 1) * P, :].rearrange("(c p) n -> p c n", p=P)
                nc.sync.dma_start(dst, res[first][:])

        close(1, 1)
        gather_tab2_words(1, 2, 4)
        close(1, 2)
        close(1, 3)
        for c0 in (4, 6):
            gather_tab2_words(1, c0, c0 + 2)
            for c in (c0, c0 + 1):
                out_pass(acc[c][:], 1, c, every, True)
            gather_tab2_words(0, c0, c0 + 2, tag="v2_w1%d" % (c0 - 4))
        for c in range(4, NT):
            close(0, c)
